import numpy as np, ml_dtypes
CORES = [35,38,43,46]
N = 4
BF = ml_dtypes.bfloat16
def gentries(a):
    return np.ascontiguousarray(a.reshape(8, 16, -1).transpose(0, 2, 1)).reshape(8, -1)
def gtable(e):
    e = np.asarray(e); return np.ascontiguousarray(e.reshape(8, -1, 16).transpose(0, 2, 1)).reshape(128, -1).astype(np.int32)
W, SB, P, HOPS, STEP, GAIN = 4096, 12, 256, 5, 1, 8
def parts(rng):
    x = rng.integers(0, 64, (N, 8, 16, W)); n = rng.integers(0, W, (N, 8, 16, W))
    s = rng.integers(0, rng.integers(2, 9, (N, 8, 1, W)) + 1, (N, 8, 16, W))
    return x, n, s, rng.integers(0, W, (N, 8, P)), rng.integers(0, 64, (N, 8, 16, P)), rng.integers(1, 256, (N, 8, 16, 1))
def lonely(rng, n, s, v, old, few, start):
    for q in range(N):
        for g in range(8):
            o = rng.permutation(W); a = o[:old]; b = o[old:old + few]
            s[q, g][:, a] = 0; n[q, g][:, b] = a[rng.integers(0, old, (16, few))]
            v[q, g, rng.permutation(P)[:start]] = b[rng.integers(0, few, start)]
def scarce(rng, n, s, v):
    lone = np.zeros((N, 8), np.int64); sh = int(rng.integers(0, 4))
    for q in range(N):
        for g in range(8):
            a, b = [int(m) for m in rng.permutation(W)[:2]]
            n[q, g][:, a] = b; s[q, g][:, b] = 0; lone[q, g] = a
    live = np.any(np.take_along_axis(s, n, 3) > 0, axis=2)
    for q in range(N):
        for g in range(8):
            c = np.flatnonzero(live[q, g])
            v[q, g] = np.where(live[q, g, v[q, g]], v[q, g], c[rng.integers(0, len(c), P)])
        for m in rng.permutation(8 * P)[:(q + sh) & 3]:
            g = int(m) // P; v[q, g, int(m) - g * P] = lone[q, g]
def plant(rng, x, n, s, v, z):
    for q in range(N):
        for g in range(8):
            o = [int(m) for m in 1 + rng.permutation(W - 1)[:25]]; X, M, S, Z = x[q, g], n[q, g], s[q, g], z[q, g]
            a, b, c = o[:3]
            M[:, 0] = c; S[:, c] = 0; Z[:, 0] = 0; v[q, g, 0] = 0
            M[:, a] = b; M[:, b] = 0; S[:, b] = rng.integers(1, 9, 16); v[q, g, 1] = a
            for p, j in ((2, 3), (P - 1, 9)):
                a, b, c, d1, d2, d3 = o[j:j + 6]; r = 63 * rng.integers(0, 2, 16)
                Z[:, p] = r; v[q, g, p] = a; M[:, a] = c; M[0, a] = b
                S[:, b] = rng.integers(1, 9, 16); S[15, b] = 0; M[0, b] = d3
                S[:, c] = rng.integers(1, 9, 16); M[:, c] = d1; M[15, c] = d2
                X[:, d1] = r; X[:, d2] = r; X[:, d3] = r; X[15, d1] = r[15] ^ 1
            for p, j in ((3, 15), (P - 2, 20)):
                a, b, c, d, h = o[j:j + 5]; r = 63 * rng.integers(0, 2, 16); k = int(rng.integers(1, 16))
                Z[:, p] = r; v[q, g, p] = a; M[:, a] = c; M[0, a] = b
                S[:, b] = rng.integers(1, 9, 16); S[0, b] = 0; M[0, b] = d; X[:, d] = r
                S[:, c] = 0; S[k, c] = int(rng.integers(1, 9)); M[k, c] = h; X[:, h] = 63 - r
def pack(x, e, v, z, w):
    return {"xs": np.ascontiguousarray(x.reshape(N, 128, W)).astype(np.float32).astype(BF), "en": np.ascontiguousarray(e.reshape(N, 128, W)).astype(np.int32),
            "v0": np.stack([gtable(a) for a in v]), "z0": np.ascontiguousarray(z.reshape(N, 128, P)).astype(np.float32).astype(BF), "wt": np.ascontiguousarray(w.reshape(N, 128, 1)).astype(np.int32)}
def setup_inputs(rng):
    x, n, s, v, z, w = parts(rng)
    lonely(rng, n, s, v, W // 8, W // 16, P // 8)
    return pack(x, n + W * s, v, z, w)
def setup_inputs_spread(rng):
    x, n, s, v, z, w = parts(rng)
    ex = rng.choice(np.array([0.25, 1.0, 4.0]), (N, 8, 1, W)); es = rng.choice(np.array([0.25, 1.0, 4.0]), (N, 8, 1, W)); en = rng.choice(np.array([1.0, 3.0]), (N, 8, 1, W))
    x = (64 * rng.random(x.shape) ** ex).astype(np.int64); s = (9 * rng.random(x.shape) ** es).astype(np.int64); n = (W * rng.random(x.shape) ** en).astype(np.int64)
    x = np.minimum(x, 63); s = np.minimum(s, 8); n = np.minimum(n, W - 1)
    v = np.minimum((W * rng.random(v.shape) ** 2).astype(np.int64), W - 1)
    z = np.minimum((64 * rng.random(z.shape) ** rng.choice(np.array([0.25, 1.0, 4.0]), (N, 8, 1, P))).astype(np.int64), 63)
    w = np.minimum(1 + (255 * rng.random(w.shape) ** 4).astype(np.int64), 255)
    scarce(rng, n, s, v)
    return pack(x, n + W * s, v, z, w)
def setup_inputs_ends(rng):
    x, n, s, v, z, w = parts(rng); hi = 9 * W - 1
    x = 63 * rng.integers(0, 2, x.shape); z = 63 * rng.integers(0, 2, z.shape); w = 1 + 254 * rng.integers(0, 2, w.shape); v = (W - 1) * rng.integers(0, 2, v.shape)
    e = np.where(rng.random(x.shape) < 0.8, hi * rng.integers(0, 2, x.shape), rng.choice(np.array([1, W - 2, 8 * W, 8 * W + 1, 9 * W - 2]), x.shape))
    e[..., W - 1] = rng.choice(np.array([hi, hi, 8 * W + 1, 9 * W - 2]), (N, 8, 16)); e[:, :, 15, W - 1] = hi
    e[..., W - 3] = 0; e[:, 7, :, W - 4] = hi
    one = rng.integers(0, 16, (N, 8)); one[:, 7] = 15; one[N - 1] = 15
    e[..., 0] = np.where(np.arange(16) == one[..., None], hi, 0)
    full = 63 * rng.integers(0, 2, (N, 8, 1)); full[:, 7] = 63
    for c in (1, W - 2, W - 1): x[..., c] = full
    for p in (0, P - 1): z[..., p] = full
    for p in (1, P - 2, P - 3): z[..., p] = 63 - full
    for p in (0, 1, P - 2, P - 1): v[..., p] = W - 1
    v[..., 2] = 0; v[..., P - 3] = W - 3; w[:, 7] = 255; w[:, 0, 0] = 1
    return pack(x, e, v, z, w)
def setup_inputs_corners(rng):
    x, n, s, v, z, w = parts(rng); o = [int(a) for a in rng.permutation(8)]; col = np.arange(W); i = np.arange(16)[:, None]
    n[:, o[0]] = col
    k = rng.integers(0, 4, (N, 16, W))
    n[:, o[1]] = np.where(k == 0, 0, np.where(k == 1, W - 1, np.where(k == 2, col, (col + 1) & (W - 1))))
    h = P // 2; s[:, o[2]] = 0; w[:, o[2], 0] = 255; w[:, o[2], 1] = W // 256 - 1
    z[:, o[2], :, :h] = 0; z[:, o[2], 0, :h] = W // 256; z[:, o[2], 1, :h] = 1
    s[:, o[3]] = np.where(i < 8, i + 1, 0)
    s[:, o[4]] = np.where(i == 0, 4, np.where(i == 12, 6, np.where(i == 13, 8, 0)))
    s[:, o[5]] = np.where(i == 0, 4, np.where(i == 13, 8, 0))
    for c in (3, 4, 5): x[:, o[c]] = np.repeat(x[:, o[c], :, :1], W, axis=2)
    s[::2, o[6]] = 8; s[1::2, o[6]] = 0
    v[..., 0] = W - 1; v[..., 1] = 0; v[..., P - 1] = W - 1
    for q in range(N):
        m = rng.permutation(W - 1); a = np.append(m[:P - 1], W - 1); b = m[P - 1:2 * P - 1]
        n[q, o[7]][:, a] = b; n[q, o[7]][:, b] = b; s[q, o[7]][:, b] = rng.integers(1, 9, (16, P)); v[q, o[7]] = a
    return pack(x, n + W * s, v, z, w)
def setup_inputs_crowd(rng):
    x, n, s, v, z, w = parts(rng)
    lonely(rng, n, s, v, W // 4, W // 4, 1)
    want = (8 * P, 8 * P - 1, 255, 256); sh = int(rng.integers(0, 4))
    for q in range(N):
        bad = np.zeros(8 * P, bool); bad[rng.permutation(8 * P)[:want[(q + sh) % 4]]] = True; bad = bad.reshape(8, P)
        for g in range(8):
            a, b, c, d, hub = [int(m) for m in rng.permutation(W)[:5]]
            n[q, g, :, a] = b; s[q, g, :, b] = 8
            if g % 3 == 0: n[q, g, :, b] = a
            if g % 3 == 1: n[q, g, :, b] = hub
            n[q, g, :, c] = d; s[q, g, :, d] = 0
            v[q, g] = np.where(bad[g], c, a)
    z[:, ::2] = np.repeat(z[:, ::2, :, :1], P, axis=3)
    return pack(x, n + W * s, v, z, w)
def setup_inputs_ties(rng):
    x, n, s, v, z, w = parts(rng)
    base = rng.integers(0, 16, (N, 8, 16, 1)); proto = rng.integers(0, 4, (N, 8, W))
    x = np.repeat(base, W, axis=3); x[:, :, 0] = base[:, :, 0] + GAIN * proto
    i = np.arange(16)[:, None]; s = (i + rng.integers(0, 8, (N, 8, 1, W))) & 7
    s = np.where((rng.random((N, 8, 1, W)) < 0.5) & (s == 0) & (i < 8), 8, s)
    n = np.where(rng.random((N, 8, 1, W)) < 0.3, rng.integers(0, W, (N, 8, 1, W)), n)
    z[:, :, 0] = 63 * (rng.random((N, 8, P)) < 0.25)
    plant(rng, x, n, s, v, z)
    return pack(x, n + W * s, v, z, w)
def check_inputs(d):
    bad = []
    for k, lo, hi in (("xs", 0, 63), ("en", 0, 9 * W - 1), ("v0", 0, W - 1), ("z0", 0, 63), ("wt", 1, 255)):
        a = np.asarray(d[k]).astype(np.float64)
        if not (np.min(a) >= lo and np.max(a) <= hi): bad.append("range of " + k)
        elif np.any(a != np.floor(a)): bad.append("whole numbers of " + k)
    return bad
def reference(xs, en, v0, z0, wt):
    x = xs.astype(np.float32).astype(np.int64).reshape(N, 8, 16, W); e = en.astype(np.int64).reshape(N, 8, 16, W); w = wt.astype(np.int64).reshape(N, 8, 16, 1)
    v = np.stack([gentries(a) for a in v0]).astype(np.int64); z = z0.astype(np.float32).astype(np.int64).reshape(N, 8, 16, P)
    tau = np.zeros((N, 8, P), np.int64); A = np.zeros(N, np.int64); k16 = np.arange(16); pn = np.arange(P)
    qi = np.arange(N)[:, None, None]; gi = np.arange(8)[None, :, None]
    for t in range(HOPS):
        if t > 0: v = np.roll(v, STEP, axis=0); tau = np.roll(tau, STEP, axis=0); z = np.roll(z, STEP, axis=0)
        ring = np.take_along_axis(e, v[:, :, None, :], 3) & (W - 1)
        F = np.take_along_axis(e, ring.reshape(N, 8, 1, 16 * P), 3).reshape(N, 8, 16, 16, P)
        newer = np.count_nonzero((F >> SB) > tau[:, :, None, None, :], axis=2)
        fk = F[:, :, (k16 + t) & 15, k16]
        rec = np.take_along_axis(x, (fk & (W - 1)).reshape(N, 8, 1, 16 * P), 3).reshape(N, 8, 16, 16, P)
        score = np.add.reduce(np.abs(rec - z[:, :, :, None, :]), axis=2) - GAIN * newer
        ok = (k16[:, None] < 16 - tau[:, :, None, :]) & ((fk >> SB) > tau[:, :, None, :])
        best = np.argmin(np.where(ok, score, 2 ** 20), axis=2); found = np.any(ok, axis=2)
        fa = np.take_along_axis(fk, best[:, :, None, :], 2)[:, :, 0]
        u = np.add.reduce(w * z, axis=2) & (W - 1)
        f = np.where(found, fa & (W - 1), ((u * u >> 5) + 37 * u + A[:, None, None]) & (W - 1))
        tau = np.where(found, fa >> SB, 0)
        z = np.where(found[:, :, None, :], z, np.abs(z - np.take_along_axis(x, f[:, :, None, :], 3)))
        A = np.count_nonzero(np.logical_not(found), axis=(1, 2)) & 255
        first = np.full((N, 8, W), P, np.int64)
        np.minimum.at(first, (qi, gi, np.concatenate([v, f], axis=2)), np.concatenate([pn, pn])[None, None, :])
        stands = (f != v) & (np.take_along_axis(first, v, 2) == pn) & (np.take_along_axis(first, f, 2) == pn)
        q, g, p = np.nonzero(stands); a = v[q, g, p]; b = f[q, g, p]
        ca = e[q, g, :, a]; cb = e[q, g, :, b]
        na = np.where(k16 % 2 == 0, cb, ca); nb = np.where(k16 % 2 == 0, ca, cb)
        na[:, 15] = b + W * (9 + t); nb[:, 15] = a + W * (9 + t)
        e[q, g, :, a] = na; e[q, g, :, b] = nb
        v = f
    return {"ys": np.add.reduce(e * (k16[:, None] + 1), axis=2).astype(np.float32), "yp": (v + W * tau).astype(np.float32), "yz": z.reshape(N, 128, P).astype(np.float32).astype(BF)}

@@ -1,0 +1,614 @@
+import numpy as np
+from concourse.bass import DstId, RemoteDMATransfer
+from concourse.mybir import AluOpType as ALU, ActivationFunctionType as ACT
+
+N, W, P, HOPS = 4, 4096, 256, 5
+F32, BF, I32, F16, U16 = "float32", "bfloat16", "int32", "float16", "uint16"
+BIG = 20480.0
+FAILKEY = 16896.0
+FV0 = 38
+XV1 = 12
+NA = 8
+ENCH = 8
+YS0 = 24
+
+SCRATCH = {
+    "eni": ("sbuf", [128, W], I32), "ring": ("sbuf", [128, W + 1024], F32), "xt": ("sbuf", [128, W + 16], BF),
+    "S": ("sbuf", [128, W + 1024], F32),
+    "v0i": ("sbuf", [128, 16], I32), "wti": ("sbuf", [128, 4], I32),
+    "LU": ("sbuf", [128, 16 * HOPS], U16), "LH": ("sbuf", [128, 16 * HOPS], F16), "LZ": ("sbuf", [128, 512 * HOPS], BF),
+    "MU": ("sbuf", [128, 32 * HOPS], U16), "MH": ("sbuf", [128, 32 * HOPS], F16), "MZ": ("sbuf", [128, 512 * HOPS], BF),
+    "v0h": ("sbuf", [128, 16], F16),
+    "F": ("sbuf", [128, W], F32), "X": ("sbuf", [128, W], BF), "CMP": ("sbuf", [128, W], BF), "MX": ("sbuf", [128, W], BF),
+    "RI": ("sbuf", [128, 256], I32), "RA": ("sbuf", [128, 256], I32), "nU": ("sbuf", [128, 256], U16),
+    "aU": ("sbuf", [128, 256], U16), "EI": ("sbuf", [128, 16, 19], I32), "NA": ("sbuf", [128, 256], I32),
+    "NH": ("sbuf", [128, 256], F16), "DE": ("sbuf", [128, 288], F32), "run": ("sbuf", [128, 288], F32),
+    "ne": ("sbuf", [128, 288], F32), "win": ("sbuf", [128, 288], F32), "MR": ("sbuf", [128, 256], F32),
+    "Lm": ("sbuf", [128, 256], BF), "FV": ("sbuf", [128, 2 * HOPS, 256], F16), "VF": ("sbuf", [128, 32], F32),
+    "EQ1": ("sbuf", [128, 32, 256], BF), "EQ2": ("sbuf", [128, 16, 256], BF),
+    "Rv": ("sbuf", [128, 256], F32), "RF": ("sbuf", [128, 512], F32), "AB": ("sbuf", [128, 512], F32),
+    "XF": ("sbuf", [128, 256], BF), "O1": ("sbuf", [128, 256], F16), "bd": ("sbuf", [128, 256], F16),
+    "bd2": ("sbuf", [128, 16], F32), "off": ("sbuf", [128, 32], F32), "offU": ("sbuf", [128, 32], U16),
+    "WI": ("sbuf", [128, 16], I32), "fI": ("sbuf", [128, 16], I32), "EW": ("sbuf", [128, 16], F32),
+    "u0": ("sbuf", [128, 16], I32), "u1": ("sbuf", [128, 16], I32), "u2": ("sbuf", [128, 16], I32),
+    "u3": ("sbuf", [128, 16], I32), "u4": ("sbuf", [128, 16], I32), "u5": ("sbuf", [128, 16], I32),
+    "flag": ("sbuf", [128, 16], BF), "a0": ("sbuf", [128, 4], I32), "a1": ("sbuf", [128, 4], I32), "Acol": ("sbuf", [128, 4], F32),
+    "YT": ("sbuf", [128, 256], F32), "YS": ("sbuf", [128, 256], F32), "YP": ("sbuf", [128, 256], F32),
+    "one32": ("sbuf", [128, 144], F32), "I32": ("sbuf", [128, 128], F32),
+    "Ibf": ("sbuf", [128, 128], BF), "nIbf": ("sbuf", [128, 128], BF), "Bt": ("sbuf", [128, 144], F32),
+    "B32": ("sbuf", [128, 128], F32), "B18": ("sbuf", [128, 8, 18], F32), "T18": ("sbuf", [128, 8, 18], F32),
+    "Bt2": ("sbuf", [128, 144], F32), "tS": ("sbuf", [128, 128], F32), "tE": ("sbuf", [128, 128], F32),
+    "TriS": ("sbuf", [128, 128], BF), "TriE": ("sbuf", [128, 128], BF), "B8k": ("sbuf", [128, 128], BF),
+    "Sel": ("sbuf", [128, 2048], BF), "rmi": ("sbuf", [128, 256], I32), "rmj": ("sbuf", [128, 256], I32),
+    "Rm": ("sbuf", [128, 256], F32), "dcol": ("sbuf", [128, 256], F32), "Dm": ("sbuf", [128, 256], F32),
+    "c1": ("sbuf", [128, 128], F32), "c2": ("sbuf", [128, 128], F32), "WC": ("sbuf", [128, 128], BF),
+    "B32m": ("sbuf", [128, 8], BF), "B16n": ("sbuf", [128, 8], BF), "B16p": ("sbuf", [128, 8], BF),
+    "ZW0": ("sbuf", [128, 8, 18], BF), "ZW1": ("sbuf", [128, 8, 18], BF), "LW": ("sbuf", [128, 8, 18], BF),
+    "SEG": ("sbuf", [128, 144], F32), "SG16": ("sbuf", [128, 256], F16), "pi": ("sbuf", [128, 4], I32), "pj": ("sbuf", [128, 4], I32),
+    "pk": ("sbuf", [128, 4], I32), "col": ("sbuf", [128, 16], F32), "Me": ("sbuf", [128, 128], F32), "Mo": ("sbuf", [128, 128], F32),
+    "M15": ("sbuf", [128, 128], BF), "wblk": ("sbuf", [128, 8], BF), "Wy": ("sbuf", [128, 8], F32),
+    "WyE": ("sbuf", [128, 128], F32), "WyO": ("sbuf", [128, 128], F32), "M16": ("sbuf", [128, 128], BF),
+    "repi": ("sbuf", [128, 16], I32), "repU": ("sbuf", [128, 16], U16), "onebf": ("sbuf", [128, 128], BF), "zbf": ("sbuf", [128, 128], BF),
+}
+for _b in range(8):
+    SCRATCH["P%d" % _b] = ("psum", [128, 512], F32)
+
+SEMAPHORES = ["eV", "eA", "eP", "eG"] + ["d%d" % i for i in range(20)] + \
+    [a + str(t) for a in ("aw", "az", "ad") for t in range(1, HOPS)] + ["sent"]
+
+
+def _mask(shape, idx):
+    m = np.zeros(shape[1:], dtype=bool)
+    m[idx[1:] if len(idx) > 1 else ...] = True
+    return int.from_bytes(np.packbits(m.reshape(-1), bitorder="little").tobytes(), "little")
+
+
+def rank_program(g, core, T, topo):
+    rank = T.rank_of(core)
+    if rank is None:
+        return
+    nxt = T.cores[(rank + 1) % N]
+    rid, pid, _se = topo.addr(nxt)
+    bits = [1 << e for e in topo.engines(core, nxt)[:8]]
+    queue = {"V": g.vector, "A": g.scalar, "P": g.tensor, "G": g, "S": g.sync}
+    ops = []
+    ndma = [0]
+    nsent = [0]
+    s_ = slice
+    al = s_(None)
+
+    def ap(name, *idx, part=al):
+        where, shape, _d = SCRATCH[name]
+        m = -1 if where == "psum" else _mask(shape, (al,) + idx)
+        return (T[name][(part,) + idx if idx else part], [(name, m)])
+
+    def c(name, a, b, st=None, part=al):
+        return ap(name, s_(a, b, st), part=part)
+
+    def ind(win, off):
+        return (win[0].indirect(off[0]), win[1] + off[1])
+
+    def add(e, fn, outs, ins, sem=None, inc=0, emit=True):
+        wr = [x for o in outs for x in o[1]]
+        rd = [x for o in ins if isinstance(o, tuple) for x in o[1]]
+        ops.append({"e": e, "fn": fn, "wr": wr, "rd": rd, "sem": sem, "inc": inc, "emit": emit})
+
+    def v(x):
+        return x[0] if isinstance(x, tuple) else x
+
+    def cp(o, i):
+        add("V", lambda: g.vector.tensor_copy(o[0], i[0]), [o], [i])
+
+    def tt(o, a, b, op):
+        add("V", lambda: g.vector.tensor_tensor(o[0], a[0], b[0], op), [o], [a, b])
+
+    def ts(o, a, s1, op0, s2=None, op1=None):
+        if op1 is None:
+            add("V", lambda: g.vector.tensor_scalar(o[0], a[0], v(s1), None, op0), [o], [a, s1])
+        else:
+            add("V", lambda: g.vector.tensor_scalar(o[0], a[0], v(s1), v(s2), op0, op1), [o], [a, s1, s2])
+
+    def ms(o, x):
+        add("V", lambda: g.vector.memset(o[0], x), [o], [])
+
+    def scan(o, d0, d1, op0, op1):
+        add("V", lambda: g.vector.tensor_tensor_scan(o[0], d0[0], d1[0], 0.0, op0, op1), [o], [d0, d1])
+
+    def act(o, i, func=ACT.Copy, scale=None, bias=None):
+        kw = {}
+        if scale is not None:
+            kw["scale"] = v(scale)
+        if bias is not None:
+            kw["bias"] = v(bias)
+        add("A", lambda: g.scalar.activation(o[0], i[0], func, **kw), [o], [i, scale, bias])
+
+    def mm(o, l, r, start=True, stop=True):
+        add("P", lambda: g.tensor.matmul(o[0], l[0], r[0], start, stop), [o], [l, r])
+
+    def iota(o, pat, base, cm, flt=False):
+        if flt:
+            add("G", lambda: g.iota(o[0], pat, base, cm, allow_small_or_imprecise_dtypes=True), [o], [])
+        else:
+            add("G", lambda: g.iota(o[0], pat, base, cm), [o], [])
+
+    def sel(o, i, pat, op, base, cm, fill=0.0):
+        add("G", lambda: g.affine_select(o[0], i[0], pat, op, fill, base, cm), [o], [i])
+
+    def dma(e, o, i):
+        sem = "d%d" % ndma[0]
+        ndma[0] += 1
+        add(e, lambda: queue[e].dma_start(o[0], i[0]).then_inc(T.sem[sem], 16), [o], [i], sem=sem, inc=16)
+
+    def send(sem, pairs):
+        n = len(bits) // len(pairs)
+        nsent[0] += len(bits)
+        add("G", lambda: g.remote_dma_fused(
+            [RemoteDMATransfer(dst_ids=[DstId(rid=rid, pnc=pid)], dma_engine_mask=sum(bits[n * j:n * j + n]),
+                               remote_sem=T.sem[sem], src=a[0], dst=b[0]) for j, (a, b) in enumerate(pairs)],
+            local_sem=T.sem.sent), [], [a for a, b in pairs], sem="sent")
+
+    def arrive(sem, bufs):
+        add("G", None, bufs, [], sem=sem, inc=8, emit=False)
+
+    def ext(t, *idx):
+        return (t[idx], [])
+
+    def weave(main, fill):
+        fill = list(fill)
+        for f in main:
+            f()
+            if fill:
+                fill.pop(0)()
+        for f in fill:
+            f()
+
+    dma("S", ap("v0i"), ext(T.v0, al))
+    dma("A", c("wti", 0, 1), ext(T.wt, al))
+    dma("A", c("LZ", 0, 256), ext(T.z0, al))
+    q = W // ENCH
+    for j in range(ENCH):
+        dma("S", c("eni", q * j, q * j + q), ext(T.en, al, s_(q * j, q * j + q)))
+    dma("S", c("xt", 0, W), ext(T.xs, al))
+
+    LMC, ME, MO, YI, WF, YE, YO, C16, BC = 0, 1, 2, 3, 4, 5, 6, 7, 8
+
+    def cl(j):
+        return c("col", j, j + 1)
+
+    b8 = c("B32", 0, 128, 16)
+    ms(ap("one32"), 1.0)
+    iota(ap("rmi"), [[0, 16], [-1, 16]], 16, 1)
+    sel(c("Bt", 0, 128), c("one32", 0, 128), [[-16, 8], [0, 16]], ALU.is_ge, 0, 1)
+    sel(ap("B32"), c("Bt", 0, 128), [[16, 8], [0, 16]], ALU.is_ge, 15, -1)
+    iota(c("pi", 0, 1), [[0, 1]], 0, 1)
+    sel(ap("I32"), c("one32", 0, 128), [[-1, 128]], ALU.is_equal, 0, 1)
+    sel(ap("tS"), ap("B32"), [[1, 128]], ALU.is_gt, 0, -1)
+    iota(ap("dcol"), [[4, 256]], W, 0, True)
+    iota(ap("T18"), [[0, 8], [1, 18]], -1, 0, True)
+    sel(ap("Bt2"), ap("one32"), [[-16, 8], [0, 18]], ALU.is_ge, 0, 1)
+    sel(ap("B18"), ap("Bt2"), [[16, 8], [0, 18]], ALU.is_ge, 15, -1)
+    sel(ap("tE"), ap("B32"), [[1, 128]], ALU.is_ge, 0, -1)
+    iota(ap("repi"), [[18, 16]], 16, 0)
+
+    ms(ap("onebf"), 1.0)
+    ms(c("xt", W, W + 16), 0.0)
+    ms(ap("SEG"), 0.0)
+    ms(ap("SG16"), 1.0)
+    ms(ap("EI"), 0)
+    ms(c("Acol", 0, 1), 0.0)
+    ms(c("P0", 256, 512), float(W))
+    ms(cl(C16), 16.0 * (W * (9 + HOPS - 1) + 2048))
+    ms(c("SEG", 0, 144, 18), 1.0e9)
+    ms(c("SG16", 0, 256, 16), 0.0)
+    ts(ap("rmj"), ap("rmi"), 15, ALU.bitwise_and)
+    ts(ap("Rm"), ap("rmj"), 0.0, ALU.is_equal)
+    for r in range(16):
+        if r < 12:
+            act(c("Sel", 128 * r, 128 * r + 128), ap("B32"), scale=c("Rm", r, r + 1))
+        else:
+            ts(c("Sel", 128 * r, 128 * r + 128), ap("B32"), c("Rm", r, r + 1), ALU.mult)
+    act(ap("B8k"), ap("B32"), scale=8192.0)
+    act(ap("TriS"), ap("tS"), scale=8192.0)
+    cp(c("LU", 0, 16), ap("v0i"))
+    ts(ap("v0h"), ap("v0i"), -2048.0, ALU.add)
+    cp(c("VF", 0, 16), ap("v0i"))
+    ts(c("pj", 0, 1), c("pi", 0, 1), 15, ALU.bitwise_and)
+    ts(c("pk", 0, 1), c("pi", 0, 1), 1, ALU.bitwise_and)
+    ts(cl(LMC), c("pj", 0, 1), -4096.0, ALU.mult, 69632.0, ALU.add)
+    ts(cl(ME), c("pk", 0, 1), 0.0, ALU.is_equal)
+    ts(cl(YI), c("pj", 0, 1), 1.0, ALU.add)
+    tt(cl(MO), c("pk", 0, 1), c("Rm", 15, 16), ALU.subtract)
+    cp(cl(WF), c("wti", 0, 1))
+    for t in range(HOPS - 1):
+        ts(cl(BC + t), c("Rm", 15, 16), float(W * (9 + t) + 2048), ALU.mult)
+    tt(cl(YE), cl(YI), cl(ME), ALU.mult)
+    tt(cl(YO), cl(YI), cl(MO), ALU.mult)
+
+    def spread(bank, o, src):
+        for r in range(16):
+            mm(c(bank, o + r, o + 256, 16), c("Sel", 128 * r, 128 * r + 128), src)
+
+    def conv(j):
+        cp(c("ring", q * j, q * j + q), c("eni", q * j, q * j + q))
+
+    def pairs(bank, eq, row, tri, start, stop, order):
+        out = []
+        for c1 in order:
+            if c1 < 15:
+                out.append(lambda c1=c1: mm(c(bank, 16 * c1 + 16, 256), ap("B8k"), ap(eq, row.start + row.step * c1, s_(16, 256 - 16 * c1)),
+                                            False, start and c1 == 14))
+            else:
+                out.append(lambda: None)
+        out.append(lambda: mm(c(bank, 0, 256), ap(tri), ap(eq, row, s_(0, 16)), start, stop and not start))
+        return out[-1:] + out[:-1] if start else out
+
+    spread("P5", 0, ap("v0h"))
+    conv(0)
+    conv(1)
+    ms(ap("T18", al, 0), FAILKEY)
+    ms(ap("T18", al, 17), 65536.0)
+    cp(ap("FV", 1, al), c("P5", 0, 256))
+    act(ap("c1"), ap("B32"), scale=-128.0)
+    sel(ap("LW"), ap("T18"), [[-16, 8], [0, 18]], ALU.is_equal, 0, 1)
+    sel(ap("LW", al, s_(1, 17)), ap("LW", al, s_(1, 17)), [[-1, 128]], ALU.not_equal, 0, 1, BIG)
+    sel(ap("WC"), ap("c1"), [[-1, 128]], ALU.not_equal, 0, 1, -128.0 - BIG)
+    act(ap("Ibf"), ap("I32"))
+    act(ap("nIbf"), ap("I32"), scale=-1.0)
+    act(ap("TriE"), ap("tE"), scale=8192.0)
+    act(ap("wblk"), b8, scale=cl(WF))
+    act(ap("B32m"), b8, scale=32.0)
+    act(ap("B16n"), b8, scale=-16.0)
+    act(ap("B16p"), b8, scale=16.0)
+    act(ap("ZW0"), ap("B18"), scale=-16.0)
+    act(ap("ZW1"), ap("B18"), scale=-16.0)
+    act(ap("Me"), ap("I32"), scale=cl(ME))
+    act(ap("Mo"), ap("I32"), scale=cl(MO))
+    act(ap("M15"), ap("I32"), scale=c("Rm", 15, 16))
+    act(ap("Wy"), b8, scale=cl(YI))
+    act(ap("WyE"), ap("B32"), scale=cl(YE))
+    act(ap("WyO"), ap("B32"), scale=cl(YO))
+    act(ap("M16"), c("Sel", 128 * 15, 128 * 16), scale=16.0)
+
+    up, down = list(range(16)), list(range(15, -1, -1))
+    pm = pairs("P2", "EQ2", s_(0, 16, 1), "TriS", True, True, up)
+    for c1 in up:
+        ts(ap("EQ2", c1, s_(0, 256 - 16 * c1)), ap("FV", 1, s_(16 * c1, 256)), 2048.0, ALU.add, c("VF", c1, c1 + 1), ALU.is_equal)
+    for f in pm:
+        f()
+    act(c("LZ", 256, 512), c("P2", 0, 256))
+    conv(2)
+    tt(ap("Dm"), ap("Rm"), ap("dcol"), ALU.mult)
+    conv(3)
+    cp(ap("repU"), ap("repi"))
+    ms(ap("ZW0", al, s_(0, 18, 17)), 0.0)
+    ms(ap("ZW1", al, 0), 0.0)
+    ms(ap("ZW1", al, s_(17 - NA, 18)), 0.0)
+    for j in range(4, ENCH):
+        conv(j)
+
+    ringw = c("ring", 0, W)
+    xw = c("xt", 0, W + 16)
+
+    for t in range(HOPS):
+        last = t == HOPS - 1
+        zc = 512 * t
+        vU = 16 * t
+        mU = 32 * t
+        zz = c("LZ", zc, zc + 256)
+        Fb, Vb = ap("FV", 2 * t, al), ap("FV", 2 * t + 1, al)
+        if t > 0:
+            arrive("aw%d" % t, [c("LU", vU, vU + 16), c("LH", vU, vU + 16)])
+            arrive("az%d" % t, [zz, Vb])
+            arrive("ad%d" % t, [c("LZ", zc + 256, zc + 512)])
+            spread("P0", 256, c("LH", vU, vU + 16))
+
+        def half(name, h, k):
+            return c(name, 2048 * h + k, 2048 * h + 2048, 16)
+
+        def blk(name, h, k, n=1):
+            return c(name, 2048 * h + 128 * k, 2048 * h + 128 * (k + n))
+
+        def hc(name, h, w=128, o=0):
+            return c(name, o + w * h, o + w * h + w)
+
+        def gat(e, dst, win, lst, a, b):
+            if e == "V":
+                cp(c(dst, 16 * a, 16 * b), ind(win, c(lst, a, b)))
+            else:
+                act(c(dst, 16 * a, 16 * b), ind(win, c(lst, a, b)))
+
+        def ysum(a, b):
+            for j in range(a, b):
+                mm(c("P7", j, 256, 32), c("ring", 128 * j, 128 * j + 128), ap("Wy"))
+
+        mm(c("P1", 0, 256), ap("Ibf"), zz)
+        for h in range(2):
+            mm(hc("P1", h, 8, 256), hc("LZ", h, 128, zc), ap("wblk"))
+        nop = lambda: None
+        af = [nop] * 4
+        if t > 0:
+            af = [lambda: cp(c("a0", 0, 1), c("P6", 300, 301)), lambda: ts(c("a1", 0, 1), c("a0", 0, 1), 255, ALU.bitwise_and),
+                  lambda: cp(c("Acol", 0, 1), c("a1", 0, 1)), lambda: cp(c("VF", 0, 16), c("LU", vU, vU + 16))]
+        uf = [lambda: cp(ap("u0"), c("P1", 256, 272)), lambda: ts(ap("u1"), ap("u0"), W - 1, ALU.bitwise_and),
+              lambda: tt(ap("u2"), ap("u1"), ap("u1"), ALU.mult),
+              lambda: ts(ap("u3"), ap("u1"), 37.0, ALU.mult, c("Acol", 0, 1), ALU.add),
+              lambda: ts(ap("u4"), ap("u2"), 5, ALU.logical_shift_right), lambda: tt(ap("u5"), ap("u3"), ap("u4"), ALU.add),
+              lambda: ts(ap("EI", al, 0), ap("u5"), W - 1, ALU.bitwise_and)]
+        for j, (a, b) in enumerate(((0, 64), (64, 256))):
+            cp(c("RI", a, b), ind(ringw, c("LU", vU + a // 16, vU + b // 16)))
+            af[2 * j]()
+            ts(c("RA", a, b), c("RI", a, b), W - 1, ALU.bitwise_and)
+            af[2 * j + 1]()
+            cp(c("nU", a, b), c("RA", a, b))
+            gat("A", "F", ringw, "nU", a, min(b, 128 - FV0))
+        nb, me, m15, mo = ("P0", "WyE", "M16", "WyO") if last else ("P7", "Me", "M15", "Mo")
+
+        def early_f():
+            mm(c(nb, 256, 512), ap(me), ap("Rv"), True, False)
+            mm(c(nb, 256, 512), ap(m15), Vb, False, False)
+
+        def early_v():
+            mm(c(nb, 0, 256), ap(mo), ap("Rv"), False, False)
+
+        cp(ap("Rv"), ap("RI"))
+        if not last:
+            early_f()
+            early_v()
+        uf[0]()
+        gat("V", "F", ringw, "nU", 128 - FV0, 128)
+        uf[1]()
+        ts(ap("Lm"), c("P0", 256, 512), cl(LMC), ALU.is_ge, 1.0, ALU.add)
+        gat("A", "F", ringw, "nU", 128, 256)
+        if last:
+            ysum(0, YS0)
+
+        def diag(h):
+            for k in range(16):
+                mm(c("P%d" % (2 + h), k, 128, 16), half("F", h, k), c("I32", (k + t) % 16, 128, 16))
+
+        def cmps(h):
+            for k in range(16):
+                tt(blk("CMP", h, k), half("F", h, k), c("P0", 256 + 128 * h, 384 + 128 * h), ALU.is_ge)
+
+        def names(h, fill):
+            e3 = ap("EI", s_(8 * h, 8 * h + 8), s_(1, 17))
+            weave([lambda: cp(e3, c("P%d" % (2 + h), 0, 128)),
+                   lambda: ts(hc("NA", h), e3, W - 1, ALU.bitwise_and),
+                   lambda: (ts(hc("NH", h), hc("NA", h), -2048.0, ALU.add), mm(hc("P4", h), hc("NH", h), ap("Ibf")))], fill)
+            ts(hc("aU", h), hc("P4", h), 2048.0, ALU.add)
+
+        def key_z(h):
+            mm(c("P%d" % (5 + h), 0, 144), hc("LZ", h, 128, zc), ap("ZW%d" % h), True, False)
+
+        def key_open(h):
+            kb = "P%d" % (5 + h)
+            for k in range(16):
+                mm(c(kb, 1 + k, 144, 18), blk("CMP", h, k), c("WC", (k + t) % 16, 128, 16), False, False)
+
+        def key_x(h, n):
+            for k in range(n):
+                mm(c("P%d" % (5 + h), 1 + k, 144, 18), half("X", h, k), ap("B16n"), False, False)
+
+        def key_max(h, ks, stop):
+            for k in ks:
+                tt(blk("MX", h, k), half("X", h, k), hc("P1", h), ALU.max)
+                mm(c("P%d" % (5 + h), 1 + k, 144, 18), blk("MX", h, k), ap("B32m"), False, stop and k == ks[-1])
+
+        def argmin(h, fill=()):
+            kb = c("P%d" % (5 + h), 0, 144)
+            scan(hc("run", h, 144), ap("SEG"), kb, ALU.add, ALU.min)
+            for f in fill:
+                f()
+            tt(hc("ne", h, 144), kb, hc("run", h, 144), ALU.not_equal)
+            scan(hc("win", h, 144), hc("ne", h, 144), hc("DE", h, 144), ALU.mult, ALU.add)
+            tt(hc("MR", h), ind(c("win", 0, 144 * h + 144), c("repU", 8 * h, 8 * h + 8)), hc("Rm", h), ALU.mult)
+
+        def wrap(h):
+            mm(hc("P4", h, 8, 256), hc("MR", h), b8)
+
+        def delta(h):
+            r_ = s_(8 * h, 8 * h + 8)
+            tt(hc("DE", h, 144), ap("EI", r_, s_(0, 18)), ap("EI", r_, s_(1, 19)), ALU.subtract)
+
+        key_z(0)
+        diag(0)
+        cmps(0)
+        key_open(0)
+        names(0, [uf[2], uf[3], lambda: (uf[4](), uf[5](), uf[6]())])
+        gat("A", "X", xw, "aU", 0, 128)
+        delta(0)
+        key_z(1)
+        if last:
+            ysum(YS0, YS0 + 3)
+        diag(1)
+        cmps(1)
+        key_open(1)
+        names(1, [nop, nop, lambda: delta(1)])
+        gat("A", "X", xw, "aU", 128, 256 - XV1)
+        if last:
+            ysum(YS0 + 3, 32)
+        for h in range(2):
+            mm(c("P%d" % (5 + h), 0, 144), hc("Lm", h), ap("LW"), False, False)
+        key_x(0, 16)
+        ab = [list(range(16 - NA, 16))[:4], list(range(16 - NA, 16))[4:]]
+        for j, ks in enumerate(ab):
+            for i, k in enumerate(ks):
+                mm(hc("P%d" % (2 + j), i), ap("nIbf"), hc("LZ", 1, 128, zc), i == 0, False)
+        for k in range(16):
+            key_max(0, [k], k == 15)
+            if last and k == 3:
+                early_f()
+            if last and k == 8:
+                early_v()
+        if XV1:
+            gat("V", "X", xw, "aU", 256 - XV1, 256)
+        argmin(0)
+        for j, ks in enumerate(ab):
+            for i, k in enumerate(ks):
+                mm(hc("P%d" % (2 + j), i), ap("Ibf"), half("X", 1, k), False, k == ks[-1])
+            if ks:
+                act(blk("MX", 1, ks[0], len(ks)), c("P%d" % (2 + j), 0, 128 * len(ks)), ACT.Abs)
+        key_x(1, 16 - NA)
+        key_max(1, list(range(16 - NA)), NA == 0)
+        for k in range(16 - NA, 16):
+            mm(c("P6", 1 + k, 144, 18), blk("MX", 1, k), ap("B16p"), False, k == 15)
+        wrap(0)
+        mm(c("P3", 0, 256), ap("Ibf"), c("LZ", zc + 256, zc + 512), True, False)
+        if last:
+            act(ap("YT"), c("P7", 0, 256))
+            for h in range(2):
+                mm(hc("P2", h), hc("YT", h), ap("I32"))
+            act(ap("YS"), c("P2", 0, 256))
+            dma("S", c("S", 0, W, part=s_(0, 64, 16)), hc("YS", 0))
+            dma("S", c("S", 0, W, part=s_(64, 128, 16)), hc("YS", 1))
+        argmin(1)
+        wrap(1)
+
+        ew = c("P4", 256, 272)
+        fU, zU = c("MU", mU, mU + 16), c("MU", mU + 16, mU + 32)
+        ts(ap("WI"), ew, float(W), ALU.add)
+        ts(zU, ew, float(W), ALU.min)
+        ts(ap("fI"), ap("WI"), W - 1, ALU.bitwise_and)
+        if last:
+            cp(ap("EW"), ew)
+        else:
+            act(ap("XF"), ind(xw, zU))
+            ts(ap("flag"), ap("WI"), 2.0 * W, ALU.is_lt)
+        ts(c("MH", mU, mU + 16), ap("fI"), -2048.0, ALU.add)
+        spread("P5", 0, c("MH", mU, mU + 16))
+        cp(fU, ap("fI"))
+        cp(c("VF", 16, 32), ap("fI"))
+
+        def zdiff():
+            mm(c("P6", 0, 256), ap("Ibf"), zz, True, False)
+            mm(c("P6", 0, 256), ap("nIbf"), ap("XF"), False, True)
+            act(c("MZ", zc, zc + 256), c("P6", 0, 256), ACT.Abs)
+
+        if last:
+            act(c("RF", 0, 256), ind(ringw, fU))
+            act(ap("XF"), ind(xw, zU))
+            mm(c("P0", 0, 256), ap("WyE"), c("RF", 0, 256), False, False)
+        else:
+            zdiff()
+            act(c("RF", 0, 256), ind(ringw, fU), scale=cl(ME))
+            tt(c("MH", mU + 16, mU + 32), ap("WI"), ap("fI"), ALU.subtract)
+            send("aw%d" % (t + 1), [(fU, c("LU", vU + 16, vU + 32)), (c("MH", mU + 16, mU + 32), c("LH", vU + 16, vU + 32))])
+        cp(Fb, c("P5", 0, 256))
+        if not last:
+            send("az%d" % (t + 1), [(c("MZ", zc, zc + 256), c("LZ", zc + 512, zc + 768)), (Fb, ap("FV", 2 * t + 3, al))])
+            act(c("RF", 256, 512), ind(ringw, fU), scale=cl(MO))
+
+        pf = pairs("P3", "EQ1", s_(0, 32, 2), "TriS", False, False, up)
+        pv = pairs("P3", "EQ1", s_(1, 32, 2), "TriE", False, False, up)
+        pm = pairs("P3", "EQ2", s_(0, 16, 1), "TriS", False, True, up)
+
+        def eq2(c1):
+            ts(ap("EQ2", c1, s_(0, 256 - 16 * c1)), ap("FV", 2 * t, s_(16 * c1, 256)), 2048.0, ALU.add, c("VF", c1, c1 + 1), ALU.is_equal)
+            pm[c1]()
+
+        for c1 in range(7, -1, -1):
+            eq2(c1)
+        for c1 in up:
+            ts(ap("EQ1", s_(2 * c1, 2 * c1 + 2), s_(0, 256 - 16 * c1)), ap("FV", s_(2 * t, 2 * t + 2), s_(16 * c1, 256)), 2048.0, ALU.add,
+               c("VF", 16 + c1, 17 + c1), ALU.is_equal)
+            pf[c1]()
+            pv[c1]()
+        pf[16]()
+        pv[16]()
+        for c1 in range(8, 16):
+            eq2(c1)
+        pm[16]()
+        if last:
+            mm(c("P0", 0, 256), ap("M16"), Fb, False, False)
+            mm(c("P0", 256, 512), ap("WyO"), c("RF", 0, 256), False, True)
+            act(ap("AB"), c("P0", 0, 512), ACT.Identity, bias=cl(C16))
+            zdiff()
+            dma("S", ext(T.yz, al), c("MZ", zc, zc + 256))
+            for r in range(16):
+                mm(c("P1", r, 256, 16, part=s_(0, 8)), c("I32", r, 128, 16), ap("EW"))
+            act(ap("YP", part=s_(0, 8)), c("P1", 0, 256, part=s_(0, 8)))
+            dma("A", ext(T.yp, al), ap("YP", part=s_(0, 8)))
+        else:
+            mm(c("P7", 0, 256), ap("M15"), Fb, False, True)
+            act(ap("AB"), c("P7", 0, 512), ACT.Identity, bias=cl(BC + t))
+            for f in pairs("P2", "EQ1", s_(0, 32, 2), "TriS", True, True, up):
+                f()
+            act(c("MZ", zc + 256, zc + 512), c("P2", 0, 256))
+            send("ad%d" % (t + 1), [(c("MZ", zc + 256, zc + 512), c("LZ", zc + 768, zc + 1024))])
+            for j in range(16):
+                mm(c("P6", 300, 301), ap("onebf"), c("flag", j, j + 1), j == 0, j == 15)
+        tt(ap("O1"), c("P3", 0, 256), ap("Dm"), ALU.min)
+        scan(ap("bd"), ap("SG16"), ap("O1"), ALU.mult, ALU.add)
+        bdw = c("bd", 15, 256, 16)
+        ts(ap("bd2"), bdw, 1.0 + 1.0 / W, ALU.mult)
+        tt(c("off", 0, 16), c("VF", 0, 16), bdw, ALU.max)
+        tt(c("off", 16, 32), c("VF", 16, 32), ap("bd2"), ALU.max)
+        cp(ap("offU"), ap("off"))
+        if last:
+            add("V", lambda: g.vector.tensor_copy(T.S[:].indirect(T.offU[:]), T.AB[:]), [ap("S")], [ap("offU"), ap("AB")])
+            dma("S", ext(T.ys, al), c("S", 0, W, part=s_(0, 128, 16)))
+        else:
+            add("V", lambda: g.vector.tensor_tensor(T.ring[:].indirect(T.offU[:]), T.RF[:], T.AB[:], ALU.add),
+                [ap("ring")], [ap("offU"), ap("RF"), ap("AB")])
+
+    hist = {}
+    deps = []
+    for i, o in enumerate(ops):
+        d = set()
+        for kind in ("rd", "wr"):
+            for name, m in o[kind]:
+                ps = SCRATCH[name][0] == "psum"
+                for j, e2, w2, m2 in hist.get(name, []):
+                    if j == i or not (m & m2):
+                        continue
+                    if ps:
+                        if e2 != o["e"] or (w2 and e2 != "P"):
+                            d.add(j)
+                    elif w2 or kind == "wr":
+                        d.add(j)
+        for kind in ("rd", "wr"):
+            for name, m in o[kind]:
+                h_ = hist.setdefault(name, [])
+                if kind == "wr":
+                    h_[:] = [x for x in h_ if (x[3] & ~m) or x[0] == i]
+                elif m == -1:
+                    h_[:] = [x for x in h_ if x[1] == o["e"]][-1:]
+                h_.append((i, o["e"], kind == "wr", m))
+        top = {}
+        for j in d:
+            key = ops[j]["sem"] or ops[j]["e"]
+            top[key] = max(top.get(key, -1), j)
+        deps.append(top)
+    seen = {}
+    need = set()
+    for i, o in enumerate(ops):
+        s = seen.setdefault(o["e"], {})
+        keep = {}
+        for key, j in deps[i].items():
+            if s.get(key, -1) < j:
+                s[key] = j
+                keep[key] = j
+                need.add(j)
+        deps[i] = keep
+    count = {}
+    at = {}
+    for i, o in enumerate(ops):
+        if o["sem"] is None and i in need:
+            count[o["e"]] = count.get(o["e"], 0) + 1
+            at[i] = count[o["e"]]
+    for i, o in enumerate(ops):
+        if not o["emit"]:
+            continue
+        qu = queue[o["e"]]
+        for key, j in deps[i].items():
+            if ops[j]["sem"] is None:
+                qu.wait_ge(T.sem["e" + key], at[j])
+            else:
+                qu.wait_ge(T.sem[key], ops[j]["inc"])
+        ins = o["fn"]()
+        if i in at:
+            ins.then_inc(T.sem["e" + o["e"]], 1)
+    for i, o in enumerate(ops):
+        if o["inc"] == 16 and i not in need:
+            queue[o["e"]].wait_ge(T.sem[o["sem"]], 16)
+    g.wait_ge(T.sem.sent, nsent[0])

@@ -6,11 +6,12 @@ N, W, P, HOPS = 4, 4096, 256, 5
 F32, BF, I32, F16, U16 = "float32", "bfloat16", "int32", "float16", "uint16"
 BIG = 20480.0
 FAILKEY = 16896.0
-FV0 = 38
-XV1 = 12
+FV0 = 48
+XV1 = 8
 NA = 8
-ENCH = 8
-YS0 = 24
+FE = 2
+ENCUT = [0, 1536, 2816, 3584, 4096]
+YS0 = 20
 
 SCRATCH = {
     "eni": ("sbuf", [128, W], I32), "ring": ("sbuf", [128, W + 1024], F32), "xt": ("sbuf", [128, W + 16], BF),
@@ -37,18 +38,22 @@ SCRATCH = {
     "one32": ("sbuf", [128, 144], F32), "I32": ("sbuf", [128, 128], F32),
     "Ibf": ("sbuf", [128, 128], BF), "nIbf": ("sbuf", [128, 128], BF), "Bt": ("sbuf", [128, 144], F32),
     "B32": ("sbuf", [128, 128], F32), "B18": ("sbuf", [128, 8, 18], F32), "T18": ("sbuf", [128, 8, 18], F32),
-    "Bt2": ("sbuf", [128, 144], F32), "tS": ("sbuf", [128, 128], F32), "tE": ("sbuf", [128, 128], F32),
-    "TriS": ("sbuf", [128, 128], BF), "TriE": ("sbuf", [128, 128], BF), "B8k": ("sbuf", [128, 128], BF),
+    "Bt2": ("sbuf", [128, 144], F32), "tS": ("sbuf", [128, 128], F32),
+    "AT": ("sbuf", [128, W + 512], F32), "VAL": ("sbuf", [128, 256 * HOPS], F32), "PT": ("sbuf", [128, 256], F16),
+    "PT0": ("sbuf", [128, 256], BF), "ZD": ("sbuf", [128, 256], BF),
+    "dW": ("sbuf", [128, 16], F32), "oa0": ("sbuf", [128, 16], F32), "oa1": ("sbuf", [128, 16], F32), "oaU": ("sbuf", [128, 16], U16),
+    "YA": ("sbuf", [128, 256], BF), "YZ": ("sbuf", [128, 256], BF), "Dg": ("sbuf", [128, 2048], BF), "LC": ("sbuf", [128, 8, 18], BF),
+    "TriS": ("sbuf", [128, 128], BF), "I16k": ("sbuf", [128, 128], BF), "B8k": ("sbuf", [128, 128], BF),
     "Sel": ("sbuf", [128, 2048], BF), "rmi": ("sbuf", [128, 256], I32), "rmj": ("sbuf", [128, 256], I32),
     "Rm": ("sbuf", [128, 256], F32), "dcol": ("sbuf", [128, 256], F32), "Dm": ("sbuf", [128, 256], F32),
-    "c1": ("sbuf", [128, 128], F32), "c2": ("sbuf", [128, 128], F32), "WC": ("sbuf", [128, 128], BF),
+    "c1": ("sbuf", [128, 128], F32), "WC": ("sbuf", [128, 128], BF),
     "B32m": ("sbuf", [128, 8], BF), "B16n": ("sbuf", [128, 8], BF), "B16p": ("sbuf", [128, 8], BF),
     "ZW0": ("sbuf", [128, 8, 18], BF), "ZW1": ("sbuf", [128, 8, 18], BF), "LW": ("sbuf", [128, 8, 18], BF),
     "SEG": ("sbuf", [128, 144], F32), "SG16": ("sbuf", [128, 256], F16), "pi": ("sbuf", [128, 4], I32), "pj": ("sbuf", [128, 4], I32),
     "pk": ("sbuf", [128, 4], I32), "col": ("sbuf", [128, 16], F32), "Me": ("sbuf", [128, 128], F32), "Mo": ("sbuf", [128, 128], F32),
     "M15": ("sbuf", [128, 128], BF), "wblk": ("sbuf", [128, 8], BF), "Wy": ("sbuf", [128, 8], F32),
     "WyE": ("sbuf", [128, 128], F32), "WyO": ("sbuf", [128, 128], F32), "M16": ("sbuf", [128, 128], BF),
-    "repi": ("sbuf", [128, 16], I32), "repU": ("sbuf", [128, 16], U16), "onebf": ("sbuf", [128, 128], BF), "zbf": ("sbuf", [128, 128], BF),
+    "repi": ("sbuf", [128, 16], I32), "repU": ("sbuf", [128, 16], U16), "onebf": ("sbuf", [128, 128], BF),
 }
 for _b in range(8):
     SCRATCH["P%d" % _b] = ("psum", [128, 512], F32)
@@ -162,12 +167,11 @@ def rank_program(g, core, T, topo):
         for f in fill:
             f()
 
-    dma("S", ap("v0i"), ext(T.v0, al))
-    dma("A", c("wti", 0, 1), ext(T.wt, al))
-    dma("A", c("LZ", 0, 256), ext(T.z0, al))
-    q = W // ENCH
-    for j in range(ENCH):
-        dma("S", c("eni", q * j, q * j + q), ext(T.en, al, s_(q * j, q * j + q)))
+    dma("A", ap("v0i"), ext(T.v0, al))
+    for a, b in zip(ENCUT, ENCUT[1:]):
+        dma("S", c("eni", a, b), ext(T.en, al, s_(a, b)))
+    dma("S", c("wti", 0, 1), ext(T.wt, al))
+    dma("S", c("LZ", 0, 256), ext(T.z0, al))
     dma("S", c("xt", 0, W), ext(T.xs, al))
 
     LMC, ME, MO, YI, WF, YE, YO, C16, BC = 0, 1, 2, 3, 4, 5, 6, 7, 8
@@ -187,10 +191,10 @@ def rank_program(g, core, T, topo):
     iota(ap("T18"), [[0, 8], [1, 18]], -1, 0, True)
     sel(ap("Bt2"), ap("one32"), [[-16, 8], [0, 18]], ALU.is_ge, 0, 1)
     sel(ap("B18"), ap("Bt2"), [[16, 8], [0, 18]], ALU.is_ge, 15, -1)
-    sel(ap("tE"), ap("B32"), [[1, 128]], ALU.is_ge, 0, -1)
     iota(ap("repi"), [[18, 16]], 16, 0)
 
     ms(ap("onebf"), 1.0)
+    ms(ap("LW"), 0.0)
     ms(c("xt", W, W + 16), 0.0)
     ms(ap("SEG"), 0.0)
     ms(ap("SG16"), 1.0)
@@ -214,11 +218,10 @@ def rank_program(g, core, T, topo):
     cp(c("VF", 0, 16), ap("v0i"))
     ts(c("pj", 0, 1), c("pi", 0, 1), 15, ALU.bitwise_and)
     ts(c("pk", 0, 1), c("pi", 0, 1), 1, ALU.bitwise_and)
-    ts(cl(LMC), c("pj", 0, 1), -4096.0, ALU.mult, 69632.0, ALU.add)
+    ts(cl(LMC), c("pj", 0, 1), 4096.0, ALU.mult, 2048.0 - 17 * W, ALU.add)
     ts(cl(ME), c("pk", 0, 1), 0.0, ALU.is_equal)
     ts(cl(YI), c("pj", 0, 1), 1.0, ALU.add)
     tt(cl(MO), c("pk", 0, 1), c("Rm", 15, 16), ALU.subtract)
-    cp(cl(WF), c("wti", 0, 1))
     for t in range(HOPS - 1):
         ts(cl(BC + t), c("Rm", 15, 16), float(W * (9 + t) + 2048), ALU.mult)
     tt(cl(YE), cl(YI), cl(ME), ALU.mult)
@@ -229,7 +232,7 @@ def rank_program(g, core, T, topo):
             mm(c(bank, o + r, o + 256, 16), c("Sel", 128 * r, 128 * r + 128), src)
 
     def conv(j):
-        cp(c("ring", q * j, q * j + q), c("eni", q * j, q * j + q))
+        cp(c("ring", ENCUT[j], ENCUT[j + 1]), c("eni", ENCUT[j], ENCUT[j + 1]))
 
     def pairs(bank, eq, row, tri, start, stop, order):
         out = []
@@ -243,19 +246,23 @@ def rank_program(g, core, T, topo):
         return out[-1:] + out[:-1] if start else out
 
     spread("P5", 0, ap("v0h"))
-    conv(0)
-    conv(1)
     ms(ap("T18", al, 0), FAILKEY)
     ms(ap("T18", al, 17), 65536.0)
     cp(ap("FV", 1, al), c("P5", 0, 256))
     act(ap("c1"), ap("B32"), scale=-128.0)
-    sel(ap("LW"), ap("T18"), [[-16, 8], [0, 18]], ALU.is_equal, 0, 1)
-    sel(ap("LW", al, s_(1, 17)), ap("LW", al, s_(1, 17)), [[-1, 128]], ALU.not_equal, 0, 1, BIG)
+    sel(ap("LC"), ap("T18"), [[-16, 8], [0, 18]], ALU.is_equal, 0, 1)
+    sel(ap("LC", al, s_(1, 17)), ap("LC", al, s_(1, 17)), [[-16, 8], [0, 16]], ALU.not_equal, -1, 1, 1.5 * BIG)
     sel(ap("WC"), ap("c1"), [[-1, 128]], ALU.not_equal, 0, 1, -128.0 - BIG)
+    iota(ap("dW"), [[16, 16]], W, 1, True)
+    iota(ap("PT0"), [[-1, 256]], 256, 0, True)
+    iota(c("AT", 0, W), [[0, W]], 0, 0, True)
+    iota(ap("VAL"), [[320, HOPS], [-1, 256]], 320, 0, True)
     act(ap("Ibf"), ap("I32"))
     act(ap("nIbf"), ap("I32"), scale=-1.0)
-    act(ap("TriE"), ap("tE"), scale=8192.0)
-    act(ap("wblk"), b8, scale=cl(WF))
+    act(ap("I16k"), ap("I32"), scale=16384.0)
+    act(ap("LW", al, s_(1, 17)), ap("I32"), scale=0.5 * BIG)
+    for r in range(8):
+        act(c("Dg", 128 * r, 128 * r + 128), ap("I32"), scale=c("Rm", r, r + 1))
     act(ap("B32m"), b8, scale=32.0)
     act(ap("B16n"), b8, scale=-16.0)
     act(ap("B16p"), b8, scale=16.0)
@@ -276,14 +283,17 @@ def rank_program(g, core, T, topo):
     for f in pm:
         f()
     act(c("LZ", 256, 512), c("P2", 0, 256))
-    conv(2)
+    conv(0)
+    for r in range(8, 16):
+        ts(c("Dg", 128 * r, 128 * r + 128), ap("Ibf"), c("Rm", r, r + 1), ALU.mult)
     tt(ap("Dm"), ap("Rm"), ap("dcol"), ALU.mult)
-    conv(3)
     cp(ap("repU"), ap("repi"))
     ms(ap("ZW0", al, s_(0, 18, 17)), 0.0)
     ms(ap("ZW1", al, 0), 0.0)
     ms(ap("ZW1", al, s_(17 - NA, 18)), 0.0)
-    for j in range(4, ENCH):
+    conv(1)
+    ts(ap("PT"), ap("PT0"), -0.5, ALU.add)
+    for j in range(2, len(ENCUT) - 1):
         conv(j)
 
     ringw = c("ring", 0, W)
@@ -321,11 +331,15 @@ def rank_program(g, core, T, topo):
             for j in range(a, b):
                 mm(c("P7", j, 256, 32), c("ring", 128 * j, 128 * j + 128), ap("Wy"))
 
-        mm(c("P1", 0, 256), ap("Ibf"), zz)
-        for h in range(2):
-            mm(hc("P1", h, 8, 256), hc("LZ", h, 128, zc), ap("wblk"))
+        def z_in():
+            mm(c("P1", 0, 256), ap("Ibf"), zz)
+            for h in range(2):
+                mm(hc("P1", h, 8, 256), hc("LZ", h, 128, zc), ap("wblk"))
+
+        if t > 0:
+            z_in()
         nop = lambda: None
-        af = [nop] * 4
+        af = [nop, nop, lambda: cp(cl(WF), c("wti", 0, 1)), lambda: (ts(ap("wblk"), b8, cl(WF), ALU.mult), z_in())]
         if t > 0:
             af = [lambda: cp(c("a0", 0, 1), c("P6", 300, 301)), lambda: ts(c("a1", 0, 1), c("a0", 0, 1), 255, ALU.bitwise_and),
                   lambda: cp(c("Acol", 0, 1), c("a1", 0, 1)), lambda: cp(c("VF", 0, 16), c("LU", vU, vU + 16))]
@@ -334,6 +348,8 @@ def rank_program(g, core, T, topo):
               lambda: ts(ap("u3"), ap("u1"), 37.0, ALU.mult, c("Acol", 0, 1), ALU.add),
               lambda: ts(ap("u4"), ap("u2"), 5, ALU.logical_shift_right), lambda: tt(ap("u5"), ap("u3"), ap("u4"), ALU.add),
               lambda: ts(ap("EI", al, 0), ap("u5"), W - 1, ALU.bitwise_and)]
+        act(ap("Lm"), c("P0", 256, 512), ACT.Sign, bias=cl(LMC))
+        act(ap("Rv"), ind(ringw, c("LU", vU, vU + 16)))
         for j, (a, b) in enumerate(((0, 64), (64, 256))):
             cp(c("RI", a, b), ind(ringw, c("LU", vU + a // 16, vU + b // 16)))
             af[2 * j]()
@@ -350,14 +366,12 @@ def rank_program(g, core, T, topo):
         def early_v():
             mm(c(nb, 0, 256), ap(mo), ap("Rv"), False, False)
 
-        cp(ap("Rv"), ap("RI"))
         if not last:
             early_f()
             early_v()
         uf[0]()
         gat("V", "F", ringw, "nU", 128 - FV0, 128)
         uf[1]()
-        ts(ap("Lm"), c("P0", 256, 512), cl(LMC), ALU.is_ge, 1.0, ALU.add)
         gat("A", "F", ringw, "nU", 128, 256)
         if last:
             ysum(0, YS0)
@@ -397,10 +411,12 @@ def rank_program(g, core, T, topo):
         def argmin(h, fill=()):
             kb = c("P%d" % (5 + h), 0, 144)
             scan(hc("run", h, 144), ap("SEG"), kb, ALU.add, ALU.min)
-            for f in fill:
-                f()
+            fill = list(fill) + [nop] * 3
+            fill[0]()
             tt(hc("ne", h, 144), kb, hc("run", h, 144), ALU.not_equal)
+            fill[1]()
             scan(hc("win", h, 144), hc("ne", h, 144), hc("DE", h, 144), ALU.mult, ALU.add)
+            fill[2]()
             tt(hc("MR", h), ind(c("win", 0, 144 * h + 144), c("repU", 8 * h, 8 * h + 8)), hc("Rm", h), ALU.mult)
 
         def wrap(h):
@@ -410,126 +426,138 @@ def rank_program(g, core, T, topo):
             r_ = s_(8 * h, 8 * h + 8)
             tt(hc("DE", h, 144), ap("EI", r_, s_(0, 18)), ap("EI", r_, s_(1, 19)), ALU.subtract)
 
-        key_z(0)
+        for h in range(2):
+            key_z(h)
+            mm(c("P%d" % (5 + h), 0, 144), hc("Lm", h), ap("LW"), False, False)
+            mm(c("P%d" % (5 + h), 0, 144), ap("onebf"), ap("LC"), False, False)
         diag(0)
         cmps(0)
         key_open(0)
         names(0, [uf[2], uf[3], lambda: (uf[4](), uf[5](), uf[6]())])
         gat("A", "X", xw, "aU", 0, 128)
         delta(0)
-        key_z(1)
-        if last:
-            ysum(YS0, YS0 + 3)
+        for r in range(16):
+            mm(c("P1", 288, 304), c("Dg", 128 * r, 128 * r + 128), c("LZ", zc + 256 + r, zc + 512, 16), r == 0, r == 15)
         diag(1)
         cmps(1)
         key_open(1)
         names(1, [nop, nop, lambda: delta(1)])
         gat("A", "X", xw, "aU", 128, 256 - XV1)
         if last:
-            ysum(YS0 + 3, 32)
-        for h in range(2):
-            mm(c("P%d" % (5 + h), 0, 144), hc("Lm", h), ap("LW"), False, False)
+            ysum(YS0, YS0 + 4)
         key_x(0, 16)
         ab = [list(range(16 - NA, 16))[:4], list(range(16 - NA, 16))[4:]]
         for j, ks in enumerate(ab):
             for i, k in enumerate(ks):
                 mm(hc("P%d" % (2 + j), i), ap("nIbf"), hc("LZ", 1, 128, zc), i == 0, False)
-        for k in range(16):
-            key_max(0, [k], k == 15)
-            if last and k == 3:
-                early_f()
-            if last and k == 8:
-                early_v()
+        key_max(0, up, True)
+        if last:
+            ysum(YS0 + 4, 32)
         if XV1:
             gat("V", "X", xw, "aU", 256 - XV1, 256)
-        argmin(0)
+        argmin(0, [lambda: tt(ap("oa0"), c("P1", 288, 304), ap("dW"), ALU.min),
+                   lambda: tt(ap("oa1"), ap("oa0"), c("VF", 0, 16), ALU.max), lambda: cp(ap("oaU"), ap("oa1"))])
         for j, ks in enumerate(ab):
             for i, k in enumerate(ks):
                 mm(hc("P%d" % (2 + j), i), ap("Ibf"), half("X", 1, k), False, k == ks[-1])
             if ks:
                 act(blk("MX", 1, ks[0], len(ks)), c("P%d" % (2 + j), 0, 128 * len(ks)), ACT.Abs)
         key_x(1, 16 - NA)
+        wrap(0)
         key_max(1, list(range(16 - NA)), NA == 0)
         for k in range(16 - NA, 16):
             mm(c("P6", 1 + k, 144, 18), blk("MX", 1, k), ap("B16p"), False, k == 15)
-        wrap(0)
         mm(c("P3", 0, 256), ap("Ibf"), c("LZ", zc + 256, zc + 512), True, False)
+        pf = pairs("P3", "EQ1", s_(0, 32, 2), "TriS", False, True, up)
+        pv = pairs("P3", "EQ1", s_(1, 32, 2), "TriS", False, False, up)
         if last:
             act(ap("YT"), c("P7", 0, 256))
+        add("A", lambda t=t: g.scalar.activation(T.AT[:].indirect(T.oaU[:]), T.VAL[:, 256 * t:256 * t + 256], ACT.Silu),
+            [ap("AT")], [ap("oaU"), c("VAL", 256 * t, 256 * t + 256)])
+
+        def eq1(c1, a, b):
+            ts(ap("EQ1", s_(2 * c1 + a, 2 * c1 + b), s_(0, 256 - 16 * c1)), ap("FV", s_(2 * t + a, 2 * t + b), s_(16 * c1, 256)),
+               2048.0, ALU.add, c("VF", 16 + c1, 17 + c1), ALU.is_equal)
+
+        ts(c("WI", 0, 8), c("P4", 256, 264), float(W), ALU.add)
+        ts(c("fI", 0, 8), c("WI", 0, 8), W - 1, ALU.bitwise_and)
+        cp(c("VF", 16, 24), c("fI", 0, 8))
+        for c1 in range(FE):
+            eq1(c1, 1, 2)
+            pv[c1]()
+        if last:
             for h in range(2):
                 mm(hc("P2", h), hc("YT", h), ap("I32"))
+            early_f()
             act(ap("YS"), c("P2", 0, 256))
-            dma("S", c("S", 0, W, part=s_(0, 64, 16)), hc("YS", 0))
-            dma("S", c("S", 0, W, part=s_(64, 128, 16)), hc("YS", 1))
+            for h in range(2):
+                dma("S", (T.S[64 * h:64 * h + 64:16, 0:W], hc("S", h, W // 2)[1]), hc("YS", h))
         argmin(1)
         wrap(1)
 
         ew = c("P4", 256, 272)
         fU, zU = c("MU", mU, mU + 16), c("MU", mU + 16, mU + 32)
-        ts(ap("WI"), ew, float(W), ALU.add)
+        ts(c("WI", 8, 16), c("P4", 264, 272), float(W), ALU.add)
         ts(zU, ew, float(W), ALU.min)
-        ts(ap("fI"), ap("WI"), W - 1, ALU.bitwise_and)
+        ts(c("fI", 8, 16), c("WI", 8, 16), W - 1, ALU.bitwise_and)
         if last:
             cp(ap("EW"), ew)
         else:
-            act(ap("XF"), ind(xw, zU))
             ts(ap("flag"), ap("WI"), 2.0 * W, ALU.is_lt)
         ts(c("MH", mU, mU + 16), ap("fI"), -2048.0, ALU.add)
         spread("P5", 0, c("MH", mU, mU + 16))
         cp(fU, ap("fI"))
-        cp(c("VF", 16, 32), ap("fI"))
+        cp(c("VF", 24, 32), c("fI", 8, 16))
 
         def zdiff():
-            mm(c("P6", 0, 256), ap("Ibf"), zz, True, False)
-            mm(c("P6", 0, 256), ap("nIbf"), ap("XF"), False, True)
-            act(c("MZ", zc, zc + 256), c("P6", 0, 256), ACT.Abs)
+            tt(ap("ZD"), zz, ap("XF"), ALU.subtract)
+            act(c("MZ", zc, zc + 256), ap("ZD"), ACT.Abs)
 
+        act(ap("YA"), ind(c("AT", 0, W), fU), ACT.Relu, bias=-float(64 + 320 * t))
         if last:
             act(c("RF", 0, 256), ind(ringw, fU))
             act(ap("XF"), ind(xw, zU))
-            mm(c("P0", 0, 256), ap("WyE"), c("RF", 0, 256), False, False)
         else:
-            zdiff()
+            act(ap("XF"), ind(xw, zU))
             act(c("RF", 0, 256), ind(ringw, fU), scale=cl(ME))
+            act(c("RF", 256, 512), ind(ringw, fU), scale=cl(MO))
             tt(c("MH", mU + 16, mU + 32), ap("WI"), ap("fI"), ALU.subtract)
             send("aw%d" % (t + 1), [(fU, c("LU", vU + 16, vU + 32)), (c("MH", mU + 16, mU + 32), c("LH", vU + 16, vU + 32))])
+        for c1 in range(FE, 8):
+            eq1(c1, 1, 2)
         cp(Fb, c("P5", 0, 256))
-        if not last:
+        for c1 in range(FE, 8):
+            pv[c1]()
+        if last:
+            early_v()
+
+        for c1 in range(8):
+            eq1(c1, 0, 1)
+            pf[c1]()
+            if c1 == 3:
+                tt(ap("YZ"), ap("YA"), ap("PT"), ALU.is_ge)
+                mm(c("P3", 0, 256), ap("I16k"), ap("YZ"), False, False)
+        zdiff()
+        if last:
+            dma("S", ext(T.yz, al), c("MZ", zc, zc + 256))
+        else:
             send("az%d" % (t + 1), [(c("MZ", zc, zc + 256), c("LZ", zc + 512, zc + 768)), (Fb, ap("FV", 2 * t + 3, al))])
-            act(c("RF", 256, 512), ind(ringw, fU), scale=cl(MO))
-
-        pf = pairs("P3", "EQ1", s_(0, 32, 2), "TriS", False, False, up)
-        pv = pairs("P3", "EQ1", s_(1, 32, 2), "TriE", False, False, up)
-        pm = pairs("P3", "EQ2", s_(0, 16, 1), "TriS", False, True, up)
-
-        def eq2(c1):
-            ts(ap("EQ2", c1, s_(0, 256 - 16 * c1)), ap("FV", 2 * t, s_(16 * c1, 256)), 2048.0, ALU.add, c("VF", c1, c1 + 1), ALU.is_equal)
-            pm[c1]()
-
-        for c1 in range(7, -1, -1):
-            eq2(c1)
-        for c1 in up:
-            ts(ap("EQ1", s_(2 * c1, 2 * c1 + 2), s_(0, 256 - 16 * c1)), ap("FV", s_(2 * t, 2 * t + 2), s_(16 * c1, 256)), 2048.0, ALU.add,
-               c("VF", 16 + c1, 17 + c1), ALU.is_equal)
+        for c1 in range(8, 16):
+            eq1(c1, 0, 2)
             pf[c1]()
             pv[c1]()
-        pf[16]()
         pv[16]()
-        for c1 in range(8, 16):
-            eq2(c1)
-        pm[16]()
+        pf[16]()
+        mm(c(nb, 0, 256), ap(m15), Fb, False, not last)
         if last:
-            mm(c("P0", 0, 256), ap("M16"), Fb, False, False)
+            mm(c("P0", 0, 256), ap("WyE"), c("RF", 0, 256), False, False)
             mm(c("P0", 256, 512), ap("WyO"), c("RF", 0, 256), False, True)
             act(ap("AB"), c("P0", 0, 512), ACT.Identity, bias=cl(C16))
-            zdiff()
-            dma("S", ext(T.yz, al), c("MZ", zc, zc + 256))
             for r in range(16):
                 mm(c("P1", r, 256, 16, part=s_(0, 8)), c("I32", r, 128, 16), ap("EW"))
             act(ap("YP", part=s_(0, 8)), c("P1", 0, 256, part=s_(0, 8)))
             dma("A", ext(T.yp, al), ap("YP", part=s_(0, 8)))
         else:
-            mm(c("P7", 0, 256), ap("M15"), Fb, False, True)
             act(ap("AB"), c("P7", 0, 512), ACT.Identity, bias=cl(BC + t))
             for f in pairs("P2", "EQ1", s_(0, 32, 2), "TriS", True, True, up):
                 f()

@@ -9,8 +9,9 @@ FAILKEY = 16896.0
 FV0 = 48
 XV1 = 8
 NA = 8
-FE = 2
-ENCUT = [0, 1536, 2816, 3584, 4096]
+FG = 2
+FE = 1
+ENCUT = [0, 1792, 3072, 3776, 4096]
 YS0 = 20
 
 SCRATCH = {
@@ -29,7 +30,7 @@ SCRATCH = {
     "EQ1": ("sbuf", [128, 32, 256], BF), "EQ2": ("sbuf", [128, 16, 256], BF),
     "Rv": ("sbuf", [128, 256], F32), "RF": ("sbuf", [128, 512], F32), "AB": ("sbuf", [128, 512], F32),
     "XF": ("sbuf", [128, 256], BF), "O1": ("sbuf", [128, 256], F16), "bd": ("sbuf", [128, 256], F16),
-    "bd2": ("sbuf", [128, 16], F32), "off": ("sbuf", [128, 32], F32), "offU": ("sbuf", [128, 32], U16),
+    "bd2": ("sbuf", [128, 32], F32), "off": ("sbuf", [128, 32], F32), "offU": ("sbuf", [128, 32], U16),
     "WI": ("sbuf", [128, 16], I32), "fI": ("sbuf", [128, 16], I32), "EW": ("sbuf", [128, 16], F32),
     "u0": ("sbuf", [128, 16], I32), "u1": ("sbuf", [128, 16], I32), "u2": ("sbuf", [128, 16], I32),
     "u3": ("sbuf", [128, 16], I32), "u4": ("sbuf", [128, 16], I32), "u5": ("sbuf", [128, 16], I32),
@@ -37,15 +38,17 @@ SCRATCH = {
     "YT": ("sbuf", [128, 256], F32), "YS": ("sbuf", [128, 256], F32), "YP": ("sbuf", [128, 256], F32),
     "one32": ("sbuf", [128, 144], F32), "I32": ("sbuf", [128, 128], F32),
     "Ibf": ("sbuf", [128, 128], BF), "nIbf": ("sbuf", [128, 128], BF), "Bt": ("sbuf", [128, 144], F32),
-    "B32": ("sbuf", [128, 128], F32), "B18": ("sbuf", [128, 8, 18], F32), "T18": ("sbuf", [128, 8, 18], F32),
-    "Bt2": ("sbuf", [128, 144], F32), "tS": ("sbuf", [128, 128], F32),
-    "AT": ("sbuf", [128, W + 512], F32), "VAL": ("sbuf", [128, 256 * HOPS], F32), "PT": ("sbuf", [128, 256], F16),
+    "B32": ("sbuf", [128, 128], F32), "T18": ("sbuf", [128, 8, 18], F32),
+    "tS": ("sbuf", [128, 128], F32),
+    "AT": ("sbuf", [128, W + 512], F32), "VAL": ("sbuf", [128, 256 * HOPS], F32), "PT": ("sbuf", [128, 256], BF),
     "PT0": ("sbuf", [128, 256], BF), "ZD": ("sbuf", [128, 256], BF),
-    "dW": ("sbuf", [128, 16], F32), "oa0": ("sbuf", [128, 16], F32), "oa1": ("sbuf", [128, 16], F32), "oaU": ("sbuf", [128, 16], U16),
+    "dW": ("sbuf", [128, 32], F32), "oa0": ("sbuf", [128, 16], F32), "oa1": ("sbuf", [128, 16], F32), "oaU": ("sbuf", [128, 16], U16),
     "YA": ("sbuf", [128, 256], BF), "YZ": ("sbuf", [128, 256], BF), "Dg": ("sbuf", [128, 2048], BF), "LC": ("sbuf", [128, 8, 18], BF),
-    "TriS": ("sbuf", [128, 128], BF), "I16k": ("sbuf", [128, 128], BF), "B8k": ("sbuf", [128, 128], BF),
+    "TriS": ("sbuf", [128, 128], BF), "B8k": ("sbuf", [128, 128], BF),
     "Sel": ("sbuf", [128, 2048], BF), "rmi": ("sbuf", [128, 256], I32), "rmj": ("sbuf", [128, 256], I32),
-    "Rm": ("sbuf", [128, 256], F32), "dcol": ("sbuf", [128, 256], F32), "Dm": ("sbuf", [128, 256], F32),
+    "Rm": ("sbuf", [128, 256], F32), "hf": ("sbuf", [128, 256], BF), "Dm": ("sbuf", [128, 256], BF),
+    "DV": ("sbuf", [128, 32], F32), "z144": ("sbuf", [128, 144], BF), "Sel2": ("sbuf", [128, 1024], BF),
+    "m8": ("sbuf", [128, 12], F32), "fH": ("sbuf", [128, 32], F16),
     "c1": ("sbuf", [128, 128], F32), "WC": ("sbuf", [128, 128], BF),
     "B32m": ("sbuf", [128, 8], BF), "B16n": ("sbuf", [128, 8], BF), "B16p": ("sbuf", [128, 8], BF),
     "ZW0": ("sbuf", [128, 8, 18], BF), "ZW1": ("sbuf", [128, 8, 18], BF), "LW": ("sbuf", [128, 8, 18], BF),
@@ -170,8 +173,8 @@ def rank_program(g, core, T, topo):
     dma("A", ap("v0i"), ext(T.v0, al))
     for a, b in zip(ENCUT, ENCUT[1:]):
         dma("S", c("eni", a, b), ext(T.en, al, s_(a, b)))
-    dma("S", c("wti", 0, 1), ext(T.wt, al))
     dma("S", c("LZ", 0, 256), ext(T.z0, al))
+    dma("S", c("wti", 0, 1), ext(T.wt, al))
     dma("S", c("xt", 0, W), ext(T.xs, al))
 
     LMC, ME, MO, YI, WF, YE, YO, C16, BC = 0, 1, 2, 3, 4, 5, 6, 7, 8
@@ -187,13 +190,15 @@ def rank_program(g, core, T, topo):
     iota(c("pi", 0, 1), [[0, 1]], 0, 1)
     sel(ap("I32"), c("one32", 0, 128), [[-1, 128]], ALU.is_equal, 0, 1)
     sel(ap("tS"), ap("B32"), [[1, 128]], ALU.is_gt, 0, -1)
-    iota(ap("dcol"), [[4, 256]], W, 0, True)
     iota(ap("T18"), [[0, 8], [1, 18]], -1, 0, True)
-    sel(ap("Bt2"), ap("one32"), [[-16, 8], [0, 18]], ALU.is_ge, 0, 1)
-    sel(ap("B18"), ap("Bt2"), [[16, 8], [0, 18]], ALU.is_ge, 15, -1)
     iota(ap("repi"), [[18, 16]], 16, 0)
+    iota(ap("PT0"), [[-1, 256]], 256, 0, True)
 
     ms(ap("onebf"), 1.0)
+    ms(ap("hf"), 0.5)
+    ms(ap("z144"), 0.0)
+    ms(ap("ZW0"), 0.0)
+    ms(ap("ZW1"), 0.0)
     ms(ap("LW"), 0.0)
     ms(c("xt", W, W + 16), 0.0)
     ms(ap("SEG"), 0.0)
@@ -248,33 +253,37 @@ def rank_program(g, core, T, topo):
     spread("P5", 0, ap("v0h"))
     ms(ap("T18", al, 0), FAILKEY)
     ms(ap("T18", al, 17), 65536.0)
+    ts(ap("Dm"), ap("Rm"), -1.0e9, ALU.mult, 1.0e9, ALU.add)
+    cp(ap("repU"), ap("repi"))
+    tt(ap("PT"), ap("PT0"), ap("Dm"), ALU.max)
     cp(ap("FV", 1, al), c("P5", 0, 256))
     act(ap("c1"), ap("B32"), scale=-128.0)
     sel(ap("LC"), ap("T18"), [[-16, 8], [0, 18]], ALU.is_equal, 0, 1)
     sel(ap("LC", al, s_(1, 17)), ap("LC", al, s_(1, 17)), [[-16, 8], [0, 16]], ALU.not_equal, -1, 1, 1.5 * BIG)
     sel(ap("WC"), ap("c1"), [[-1, 128]], ALU.not_equal, 0, 1, -128.0 - BIG)
-    iota(ap("dW"), [[16, 16]], W, 1, True)
-    iota(ap("PT0"), [[-1, 256]], 256, 0, True)
+    iota(ap("dW"), [[16, 32]], W, 1, True)
+    for r in range(16):
+        sel(c("Dg", 128 * r, 128 * r + 128), ap("I32"), [[0, 8], [1, 16]], ALU.is_equal, -r, 0)
+    iota(c("VAL", 0, 256), [[-1, 256]], 320, 0, True)
     iota(c("AT", 0, W), [[0, W]], 0, 0, True)
-    iota(ap("VAL"), [[320, HOPS], [-1, 256]], 320, 0, True)
+    iota(c("VAL", 256, 256 * HOPS), [[320, HOPS - 1], [-1, 256]], 640, 0, True)
     act(ap("Ibf"), ap("I32"))
     act(ap("nIbf"), ap("I32"), scale=-1.0)
-    act(ap("I16k"), ap("I32"), scale=16384.0)
-    act(ap("LW", al, s_(1, 17)), ap("I32"), scale=0.5 * BIG)
-    for r in range(8):
-        act(c("Dg", 128 * r, 128 * r + 128), ap("I32"), scale=c("Rm", r, r + 1))
+
+    act(ap("LW", al, s_(1, 17)), ap("I32"), ACT.Silu, scale=0.5 * BIG)
     act(ap("B32m"), b8, scale=32.0)
     act(ap("B16n"), b8, scale=-16.0)
     act(ap("B16p"), b8, scale=16.0)
-    act(ap("ZW0"), ap("B18"), scale=-16.0)
-    act(ap("ZW1"), ap("B18"), scale=-16.0)
+    act(ap("ZW0", al, s_(1, 17)), ap("B32"), scale=-16.0)
+    act(ap("ZW1", al, s_(1, 17 - NA)), c("B32", 0, 128, 16 // (16 - NA)), scale=-16.0)
     act(ap("Me"), ap("I32"), scale=cl(ME))
     act(ap("Mo"), ap("I32"), scale=cl(MO))
     act(ap("M15"), ap("I32"), scale=c("Rm", 15, 16))
-    act(ap("Wy"), b8, scale=cl(YI))
-    act(ap("WyE"), ap("B32"), scale=cl(YE))
-    act(ap("WyO"), ap("B32"), scale=cl(YO))
-    act(ap("M16"), c("Sel", 128 * 15, 128 * 16), scale=16.0)
+    tt(c("m8", 0, 8), c("Rm", 0, 8), c("Rm", 8, 16), ALU.add)
+    ts(c("m8", 8, 9), c("pj", 0, 1), 8.0, ALU.is_lt)
+    ts(c("m8", 9, 10), c("pj", 0, 1), 8.0, ALU.is_ge)
+    for r in range(8):
+        act(c("Sel2", 128 * r, 128 * r + 128), ap("B32"), scale=c("m8", r, r + 1))
 
     up, down = list(range(16)), list(range(15, -1, -1))
     pm = pairs("P2", "EQ2", s_(0, 16, 1), "TriS", True, True, up)
@@ -283,17 +292,7 @@ def rank_program(g, core, T, topo):
     for f in pm:
         f()
     act(c("LZ", 256, 512), c("P2", 0, 256))
-    conv(0)
-    for r in range(8, 16):
-        ts(c("Dg", 128 * r, 128 * r + 128), ap("Ibf"), c("Rm", r, r + 1), ALU.mult)
-    tt(ap("Dm"), ap("Rm"), ap("dcol"), ALU.mult)
-    cp(ap("repU"), ap("repi"))
-    ms(ap("ZW0", al, s_(0, 18, 17)), 0.0)
-    ms(ap("ZW1", al, 0), 0.0)
-    ms(ap("ZW1", al, s_(17 - NA, 18)), 0.0)
-    conv(1)
-    ts(ap("PT"), ap("PT0"), -0.5, ALU.add)
-    for j in range(2, len(ENCUT) - 1):
+    for j in range(len(ENCUT) - 1):
         conv(j)
 
     ringw = c("ring", 0, W)
@@ -347,7 +346,12 @@ def rank_program(g, core, T, topo):
               lambda: tt(ap("u2"), ap("u1"), ap("u1"), ALU.mult),
               lambda: ts(ap("u3"), ap("u1"), 37.0, ALU.mult, c("Acol", 0, 1), ALU.add),
               lambda: ts(ap("u4"), ap("u2"), 5, ALU.logical_shift_right), lambda: tt(ap("u5"), ap("u3"), ap("u4"), ALU.add),
-              lambda: ts(ap("EI", al, 0), ap("u5"), W - 1, ALU.bitwise_and)]
+              lambda: ts(ap("u0"), ap("u5"), W - 1, ALU.bitwise_and)]
+        if t == 1:
+            act(ap("Wy"), b8, scale=cl(YI))
+            act(ap("WyE"), ap("B32"), scale=cl(YE))
+            act(ap("WyO"), ap("B32"), scale=cl(YO))
+            act(ap("M16"), c("Sel", 128 * 15, 128 * 16), scale=16.0)
         act(ap("Lm"), c("P0", 256, 512), ACT.Sign, bias=cl(LMC))
         act(ap("Rv"), ind(ringw, c("LU", vU, vU + 16)))
         for j, (a, b) in enumerate(((0, 64), (64, 256))):
@@ -357,14 +361,15 @@ def rank_program(g, core, T, topo):
             af[2 * j + 1]()
             cp(c("nU", a, b), c("RA", a, b))
             gat("A", "F", ringw, "nU", a, min(b, 128 - FV0))
-        nb, me, m15, mo = ("P0", "WyE", "M16", "WyO") if last else ("P7", "Me", "M15", "Mo")
+        nf, me, m15, mo = ("P0", "WyE", "M16", "WyO") if last else ("P7", "Me", "M15", "Mo")
+        nb = "P7"
 
         def early_f():
-            mm(c(nb, 256, 512), ap(me), ap("Rv"), True, False)
-            mm(c(nb, 256, 512), ap(m15), Vb, False, False)
+            mm(c(nf, 256, 512), ap(me), ap("Rv"), True, False)
+            mm(c(nf, 256, 512), ap(m15), Vb, False, False)
 
         def early_v():
-            mm(c(nb, 0, 256), ap(mo), ap("Rv"), False, False)
+            mm(c(nb, 0, 256), ap(mo), ap("Rv"), last, False)
 
         if not last:
             early_f()
@@ -373,12 +378,11 @@ def rank_program(g, core, T, topo):
         gat("V", "F", ringw, "nU", 128 - FV0, 128)
         uf[1]()
         gat("A", "F", ringw, "nU", 128, 256)
-        if last:
-            ysum(0, YS0)
 
         def diag(h):
+            mm(c("P%d" % (2 + h), 0, 144), ap("onebf"), ap("z144"), True, False)
             for k in range(16):
-                mm(c("P%d" % (2 + h), k, 128, 16), half("F", h, k), c("I32", (k + t) % 16, 128, 16))
+                mm(c("P%d" % (2 + h), 1 + k, 144, 18), half("F", h, k), c("I32", (k + t) % 16, 128, 16), False, k == 15)
 
         def cmps(h):
             for k in range(16):
@@ -386,7 +390,7 @@ def rank_program(g, core, T, topo):
 
         def names(h, fill):
             e3 = ap("EI", s_(8 * h, 8 * h + 8), s_(1, 17))
-            weave([lambda: cp(e3, c("P%d" % (2 + h), 0, 128)),
+            weave([lambda: cp(ap("EI", s_(8 * h, 8 * h + 8), s_(0, 18)), c("P%d" % (2 + h), 0, 144)),
                    lambda: ts(hc("NA", h), e3, W - 1, ALU.bitwise_and),
                    lambda: (ts(hc("NH", h), hc("NA", h), -2048.0, ALU.add), mm(hc("P4", h), hc("NH", h), ap("Ibf")))], fill)
             ts(hc("aU", h), hc("P4", h), 2048.0, ALU.add)
@@ -424,38 +428,40 @@ def rank_program(g, core, T, topo):
 
         def delta(h):
             r_ = s_(8 * h, 8 * h + 8)
-            tt(hc("DE", h, 144), ap("EI", r_, s_(0, 18)), ap("EI", r_, s_(1, 19)), ALU.subtract)
+            tt(hc("DE", h, 144), c("P%d" % (2 + h), 0, 144), ap("EI", r_, s_(1, 19)), ALU.subtract)
 
         for h in range(2):
             key_z(h)
             mm(c("P%d" % (5 + h), 0, 144), hc("Lm", h), ap("LW"), False, False)
             mm(c("P%d" % (5 + h), 0, 144), ap("onebf"), ap("LC"), False, False)
+            if last and h == 0:
+                ysum(0, YS0)
         diag(0)
         cmps(0)
         key_open(0)
-        names(0, [uf[2], uf[3], lambda: (uf[4](), uf[5](), uf[6]())])
+        names(0, [uf[2], uf[3], lambda: (uf[4](), delta(0))])
         gat("A", "X", xw, "aU", 0, 128)
-        delta(0)
-        for r in range(16):
-            mm(c("P1", 288, 304), c("Dg", 128 * r, 128 * r + 128), c("LZ", zc + 256 + r, zc + 512, 16), r == 0, r == 15)
+        if last:
+            ysum(YS0, YS0 + 3)
         diag(1)
         cmps(1)
         key_open(1)
-        names(1, [nop, nop, lambda: delta(1)])
+        names(1, [uf[5], uf[6], lambda: delta(1)])
         gat("A", "X", xw, "aU", 128, 256 - XV1)
-        if last:
-            ysum(YS0, YS0 + 4)
+        tt(c("DE", 0, 288, 18), c("DE", 0, 288, 18), ap("u0"), ALU.add)
         key_x(0, 16)
+        for r in range(16):
+            mm(c("P0", 0, 16), c("Dg", 128 * r, 128 * r + 128), c("LZ", zc + 256 + r, zc + 512, 16), r == 0, r == 15)
         ab = [list(range(16 - NA, 16))[:4], list(range(16 - NA, 16))[4:]]
         for j, ks in enumerate(ab):
             for i, k in enumerate(ks):
                 mm(hc("P%d" % (2 + j), i), ap("nIbf"), hc("LZ", 1, 128, zc), i == 0, False)
         key_max(0, up, True)
         if last:
-            ysum(YS0 + 4, 32)
+            ysum(YS0 + 3, 32)
         if XV1:
             gat("V", "X", xw, "aU", 256 - XV1, 256)
-        argmin(0, [lambda: tt(ap("oa0"), c("P1", 288, 304), ap("dW"), ALU.min),
+        argmin(0, [lambda: tt(ap("oa0"), c("P0", 0, 16), c("dW", 0, 16), ALU.min),
                    lambda: tt(ap("oa1"), ap("oa0"), c("VF", 0, 16), ALU.max), lambda: cp(ap("oaU"), ap("oa1"))])
         for j, ks in enumerate(ab):
             for i, k in enumerate(ks):
@@ -464,10 +470,14 @@ def rank_program(g, core, T, topo):
                 act(blk("MX", 1, ks[0], len(ks)), c("P%d" % (2 + j), 0, 128 * len(ks)), ACT.Abs)
         key_x(1, 16 - NA)
         wrap(0)
-        key_max(1, list(range(16 - NA)), NA == 0)
+        weave([(lambda k=k: key_max(1, [k], False)) for k in range(16 - NA)],
+              [nop] * (14 - NA) + [lambda: ts(c("WI", 0, 8), c("P4", 256, 264), float(W), ALU.add),
+                                   lambda: ts(c("fI", 0, 8), c("WI", 0, 8), W - 1, ALU.bitwise_and),
+                                   lambda: cp(c("VF", 16, 24), c("fI", 0, 8))])
         for k in range(16 - NA, 16):
             mm(c("P6", 1 + k, 144, 18), blk("MX", 1, k), ap("B16p"), False, k == 15)
         mm(c("P3", 0, 256), ap("Ibf"), c("LZ", zc + 256, zc + 512), True, False)
+        mm(c("P3", 0, 256), ap("Ibf"), ap("hf"), False, False)
         pf = pairs("P3", "EQ1", s_(0, 32, 2), "TriS", False, True, up)
         pv = pairs("P3", "EQ1", s_(1, 32, 2), "TriS", False, False, up)
         if last:
@@ -479,80 +489,83 @@ def rank_program(g, core, T, topo):
             ts(ap("EQ1", s_(2 * c1 + a, 2 * c1 + b), s_(0, 256 - 16 * c1)), ap("FV", s_(2 * t + a, 2 * t + b), s_(16 * c1, 256)),
                2048.0, ALU.add, c("VF", 16 + c1, 17 + c1), ALU.is_equal)
 
-        ts(c("WI", 0, 8), c("P4", 256, 264), float(W), ALU.add)
-        ts(c("fI", 0, 8), c("WI", 0, 8), W - 1, ALU.bitwise_and)
-        cp(c("VF", 16, 24), c("fI", 0, 8))
+        def fv(c1):
+            return lambda: (eq1(c1, 1, 2), pv[c1]())
+
         for c1 in range(FE):
-            eq1(c1, 1, 2)
-            pv[c1]()
+            fv(c1)()
         if last:
             for h in range(2):
                 mm(hc("P2", h), hc("YT", h), ap("I32"))
-            early_f()
             act(ap("YS"), c("P2", 0, 256))
             for h in range(2):
                 dma("S", (T.S[64 * h:64 * h + 64:16, 0:W], hc("S", h, W // 2)[1]), hc("YS", h))
-        argmin(1)
+        argmin(1, [fv(7), fv(6), fv(5)])
         wrap(1)
+        for c1 in range(4, FG - 1, -1):
+            fv(c1)()
 
         ew = c("P4", 256, 272)
         fU, zU = c("MU", mU, mU + 16), c("MU", mU + 16, mU + 32)
         ts(c("WI", 8, 16), c("P4", 264, 272), float(W), ALU.add)
         ts(zU, ew, float(W), ALU.min)
+        act(ap("XF"), ind(xw, zU))
         ts(c("fI", 8, 16), c("WI", 8, 16), W - 1, ALU.bitwise_and)
         if last:
             cp(ap("EW"), ew)
         else:
-            ts(ap("flag"), ap("WI"), 2.0 * W, ALU.is_lt)
-        ts(c("MH", mU, mU + 16), ap("fI"), -2048.0, ALU.add)
-        spread("P5", 0, c("MH", mU, mU + 16))
+            ts(ap("flag"), zU, float(W), ALU.is_lt)
+        for j in range(2):
+            ts(c("fH", j, 32, 2), ap("fI"), -2048.0, ALU.add, c("m8", 8 + j, 9 + j), ALU.mult)
+        for r in range(8):
+            mm(c("P5", r, 256, 8), c("Sel2", 128 * r, 128 * r + 128), ap("fH"))
         cp(fU, ap("fI"))
         cp(c("VF", 24, 32), c("fI", 8, 16))
 
         def zdiff():
-            tt(ap("ZD"), zz, ap("XF"), ALU.subtract)
-            act(c("MZ", zc, zc + 256), ap("ZD"), ACT.Abs)
+            mm(c("P6", 0, 256), ap("Ibf"), zz, True, False)
+            mm(c("P6", 0, 256), ap("nIbf"), ap("XF"), False, True)
+            act(c("MZ", zc, zc + 256), c("P6", 0, 256), ACT.Abs)
 
         act(ap("YA"), ind(c("AT", 0, W), fU), ACT.Relu, bias=-float(64 + 320 * t))
-        if last:
-            act(c("RF", 0, 256), ind(ringw, fU))
-            act(ap("XF"), ind(xw, zU))
-        else:
-            act(ap("XF"), ind(xw, zU))
-            act(c("RF", 0, 256), ind(ringw, fU), scale=cl(ME))
-            act(c("RF", 256, 512), ind(ringw, fU), scale=cl(MO))
+        if not last:
             tt(c("MH", mU + 16, mU + 32), ap("WI"), ap("fI"), ALU.subtract)
             send("aw%d" % (t + 1), [(fU, c("LU", vU + 16, vU + 32)), (c("MH", mU + 16, mU + 32), c("LH", vU + 16, vU + 32))])
-        for c1 in range(FE, 8):
-            eq1(c1, 1, 2)
+        for c1 in range(FE, FG):
+            fv(c1)()
+        mm(c("P3", 0, 128), ap("TriS"), ap("EQ1", s_(1, 16, 2), s_(0, 16)), False, False)
+        tt(ap("DV"), ap("dW"), ap("VF"), ALU.subtract)
+        zdiff()
+        if last:
+            act(c("RF", 0, 256), ind(ringw, fU))
+        else:
+            act(c("RF", 0, 256), ind(ringw, fU), scale=cl(ME))
+            act(c("RF", 256, 512), ind(ringw, fU), scale=cl(MO))
         cp(Fb, c("P5", 0, 256))
-        for c1 in range(FE, 8):
-            pv[c1]()
         if last:
             early_v()
 
-        for c1 in range(8):
-            eq1(c1, 0, 1)
-            pf[c1]()
-            if c1 == 3:
-                tt(ap("YZ"), ap("YA"), ap("PT"), ALU.is_ge)
-                mm(c("P3", 0, 256), ap("I16k"), ap("YZ"), False, False)
-        zdiff()
         if last:
             dma("S", ext(T.yz, al), c("MZ", zc, zc + 256))
         else:
             send("az%d" % (t + 1), [(c("MZ", zc, zc + 256), c("LZ", zc + 512, zc + 768)), (Fb, ap("FV", 2 * t + 3, al))])
+        for c1 in range(8):
+            eq1(c1, 0, 1)
+            pf[c1]()
         for c1 in range(8, 16):
             eq1(c1, 0, 2)
             pf[c1]()
             pv[c1]()
-        pv[16]()
+        tt(ap("YZ"), ap("PT"), ap("YA"), ALU.subtract)
+        mm(c("P3", 128, 256), ap("TriS"), ap("EQ1", s_(17, 32, 2), s_(0, 16)), False, False)
         pf[16]()
         mm(c(nb, 0, 256), ap(m15), Fb, False, not last)
         if last:
-            mm(c("P0", 0, 256), ap("WyE"), c("RF", 0, 256), False, False)
+            mm(c("P7", 0, 256), ap("WyE"), c("RF", 0, 256), False, True)
+            early_f()
             mm(c("P0", 256, 512), ap("WyO"), c("RF", 0, 256), False, True)
-            act(ap("AB"), c("P0", 0, 512), ACT.Identity, bias=cl(C16))
+            act(c("AB", 0, 256), c("P7", 0, 256), ACT.Identity, bias=cl(C16))
+            act(c("AB", 256, 512), c("P0", 256, 512), ACT.Identity, bias=cl(C16))
             for r in range(16):
                 mm(c("P1", r, 256, 16, part=s_(0, 8)), c("I32", r, 128, 16), ap("EW"))
             act(ap("YP", part=s_(0, 8)), c("P1", 0, 256, part=s_(0, 8)))
@@ -565,15 +578,16 @@ def rank_program(g, core, T, topo):
             send("ad%d" % (t + 1), [(c("MZ", zc + 256, zc + 512), c("LZ", zc + 768, zc + 1024))])
             for j in range(16):
                 mm(c("P6", 300, 301), ap("onebf"), c("flag", j, j + 1), j == 0, j == 15)
-        tt(ap("O1"), c("P3", 0, 256), ap("Dm"), ALU.min)
+        tt(ap("O1"), c("P3", 0, 256), ap("YZ"), ALU.is_gt)
         scan(ap("bd"), ap("SG16"), ap("O1"), ALU.mult, ALU.add)
-        bdw = c("bd", 15, 256, 16)
-        ts(ap("bd2"), bdw, 1.0 + 1.0 / W, ALU.mult)
-        tt(c("off", 0, 16), c("VF", 0, 16), bdw, ALU.max)
-        tt(c("off", 16, 32), c("VF", 16, 32), ap("bd2"), ALU.max)
+        for h in range(2):
+            tt(hc("bd2", h, 16), c("bd", 15, 256, 16), hc("DV", h, 16), ALU.mult)
+        tt(ap("off"), ap("bd2"), ap("VF"), ALU.add)
         cp(ap("offU"), ap("off"))
         if last:
-            add("V", lambda: g.vector.tensor_copy(T.S[:].indirect(T.offU[:]), T.AB[:]), [ap("S")], [ap("offU"), ap("AB")])
+            for h in range(2):
+                add("V", lambda h=h: g.vector.tensor_copy(T.S[:].indirect(T.offU[:, 16 * h:16 * h + 16]), T.AB[:, 256 * h:256 * h + 256]),
+                    [ap("S")], [ap("offU"), hc("AB", h, 256)])
             dma("S", ext(T.ys, al), c("S", 0, W, part=s_(0, 128, 16)))
         else:
             add("V", lambda: g.vector.tensor_tensor(T.ring[:].indirect(T.offU[:]), T.RF[:], T.AB[:], ALU.add),

import numpy as np
from concourse.bass import DstId, RemoteDMATransfer
from concourse.mybir import AluOpType as ALU, ActivationFunctionType as ACT

N, W, P, HOPS = 4, 4096, 256, 5
F32, BF, I32, F16, U16 = "float32", "bfloat16", "int32", "float16", "uint16"
BIG = 20480.0
FAILKEY = 16896.0
FV0 = 48
XV1 = 8
NA = 8
FG = 2
FE = 1
ENCUT = [0, 1792, 3072, 3776, 4096]
YS0 = 20

SCRATCH = {
    "eni": ("sbuf", [128, W], I32), "ring": ("sbuf", [128, W + 1024], F32), "xt": ("sbuf", [128, W + 16], BF),
    "S": ("sbuf", [128, W + 1024], F32),
    "v0i": ("sbuf", [128, 16], I32), "wti": ("sbuf", [128, 4], I32),
    "LU": ("sbuf", [128, 16 * HOPS], U16), "LH": ("sbuf", [128, 16 * HOPS], F16), "LZ": ("sbuf", [128, 512 * HOPS], BF),
    "MU": ("sbuf", [128, 32 * HOPS], U16), "MH": ("sbuf", [128, 32 * HOPS], F16), "MZ": ("sbuf", [128, 512 * HOPS], BF),
    "v0h": ("sbuf", [128, 16], F16),
    "F": ("sbuf", [128, W], F32), "X": ("sbuf", [128, W], BF), "CMP": ("sbuf", [128, W], BF), "MX": ("sbuf", [128, W], BF),
    "RI": ("sbuf", [128, 256], I32), "RA": ("sbuf", [128, 256], I32), "nU": ("sbuf", [128, 256], U16),
    "aU": ("sbuf", [128, 256], U16), "EI": ("sbuf", [128, 16, 19], I32), "NA": ("sbuf", [128, 256], I32),
    "NH": ("sbuf", [128, 256], F16), "DE": ("sbuf", [128, 288], F32), "run": ("sbuf", [128, 288], F32),
    "ne": ("sbuf", [128, 288], F32), "win": ("sbuf", [128, 288], F32), "MR": ("sbuf", [128, 256], F32),
    "Lm": ("sbuf", [128, 256], BF), "FV": ("sbuf", [128, 2 * HOPS, 256], F16), "VF": ("sbuf", [128, 32], F32),
    "EQ1": ("sbuf", [128, 32, 256], BF), "EQ2": ("sbuf", [128, 16, 256], BF),
    "Rv": ("sbuf", [128, 256], F32), "RF": ("sbuf", [128, 512], F32), "AB": ("sbuf", [128, 512], F32),
    "XF": ("sbuf", [128, 256], BF), "O1": ("sbuf", [128, 256], F16), "bd": ("sbuf", [128, 256], F16),
    "bd2": ("sbuf", [128, 32], F32), "off": ("sbuf", [128, 32], F32), "offU": ("sbuf", [128, 32], U16),
    "WI": ("sbuf", [128, 16], I32), "fI": ("sbuf", [128, 16], I32), "EW": ("sbuf", [128, 16], F32),
    "u0": ("sbuf", [128, 16], I32), "u1": ("sbuf", [128, 16], I32), "u2": ("sbuf", [128, 16], I32),
    "u3": ("sbuf", [128, 16], I32), "u4": ("sbuf", [128, 16], I32), "u5": ("sbuf", [128, 16], I32),
    "flag": ("sbuf", [128, 16], BF), "a0": ("sbuf", [128, 4], I32), "a1": ("sbuf", [128, 4], I32), "Acol": ("sbuf", [128, 4], F32),
    "YT": ("sbuf", [128, 256], F32), "YS": ("sbuf", [128, 256], F32), "YP": ("sbuf", [128, 256], F32),
    "one32": ("sbuf", [128, 144], F32), "I32": ("sbuf", [128, 128], F32),
    "Ibf": ("sbuf", [128, 128], BF), "nIbf": ("sbuf", [128, 128], BF), "Bt": ("sbuf", [128, 144], F32),
    "B32": ("sbuf", [128, 128], F32), "T18": ("sbuf", [128, 8, 18], F32),
    "tS": ("sbuf", [128, 128], F32),
    "AT": ("sbuf", [128, W + 512], F32), "VAL": ("sbuf", [128, 256 * HOPS], F32), "PT": ("sbuf", [128, 256], BF),
    "PT0": ("sbuf", [128, 256], BF), "ZD": ("sbuf", [128, 256], BF),
    "dW": ("sbuf", [128, 32], F32), "oa0": ("sbuf", [128, 16], F32), "oa1": ("sbuf", [128, 16], F32), "oaU": ("sbuf", [128, 16], U16),
    "YA": ("sbuf", [128, 256], BF), "YZ": ("sbuf", [128, 256], BF), "Dg": ("sbuf", [128, 2048], BF), "LC": ("sbuf", [128, 8, 18], BF),
    "TriS": ("sbuf", [128, 128], BF), "B8k": ("sbuf", [128, 128], BF),
    "Sel": ("sbuf", [128, 2048], BF), "rmi": ("sbuf", [128, 256], I32), "rmj": ("sbuf", [128, 256], I32),
    "Rm": ("sbuf", [128, 256], F32), "hf": ("sbuf", [128, 256], BF), "Dm": ("sbuf", [128, 256], BF),
    "DV": ("sbuf", [128, 32], F32), "z144": ("sbuf", [128, 144], BF), "Sel2": ("sbuf", [128, 1024], BF),
    "m8": ("sbuf", [128, 12], F32), "fH": ("sbuf", [128, 32], F16),
    "c1": ("sbuf", [128, 128], F32), "WC": ("sbuf", [128, 128], BF),
    "B32m": ("sbuf", [128, 8], BF), "B16n": ("sbuf", [128, 8], BF), "B16p": ("sbuf", [128, 8], BF),
    "ZW0": ("sbuf", [128, 8, 18], BF), "ZW1": ("sbuf", [128, 8, 18], BF), "LW": ("sbuf", [128, 8, 18], BF),
    "SEG": ("sbuf", [128, 144], F32), "SG16": ("sbuf", [128, 256], F16), "pi": ("sbuf", [128, 4], I32), "pj": ("sbuf", [128, 4], I32),
    "pk": ("sbuf", [128, 4], I32), "col": ("sbuf", [128, 16], F32), "Me": ("sbuf", [128, 128], F32), "Mo": ("sbuf", [128, 128], F32),
    "M15": ("sbuf", [128, 128], BF), "wblk": ("sbuf", [128, 8], BF), "Wy": ("sbuf", [128, 8], F32),
    "WyE": ("sbuf", [128, 128], F32), "WyO": ("sbuf", [128, 128], F32), "M16": ("sbuf", [128, 128], BF),
    "repi": ("sbuf", [128, 16], I32), "repU": ("sbuf", [128, 16], U16), "onebf": ("sbuf", [128, 128], BF),
}
for _b in range(8):
    SCRATCH["P%d" % _b] = ("psum", [128, 512], F32)

SEMAPHORES = ["eV", "eA", "eP", "eG"] + ["d%d" % i for i in range(20)] + \
    [a + str(t) for a in ("aw", "az", "ad") for t in range(1, HOPS)] + ["sent"]


def _mask(shape, idx):
    m = np.zeros(shape[1:], dtype=bool)
    m[idx[1:] if len(idx) > 1 else ...] = True
    return int.from_bytes(np.packbits(m.reshape(-1), bitorder="little").tobytes(), "little")


def rank_program(g, core, T, topo):
    rank = T.rank_of(core)
    if rank is None:
        return
    nxt = T.cores[(rank + 1) % N]
    rid, pid, _se = topo.addr(nxt)
    bits = [1 << e for e in topo.engines(core, nxt)[:8]]
    queue = {"V": g.vector, "A": g.scalar, "P": g.tensor, "G": g, "S": g.sync}
    ops = []
    ndma = [0]
    nsent = [0]
    s_ = slice
    al = s_(None)

    def ap(name, *idx, part=al):
        where, shape, _d = SCRATCH[name]
        m = -1 if where == "psum" else _mask(shape, (al,) + idx)
        return (T[name][(part,) + idx if idx else part], [(name, m)])

    def c(name, a, b, st=None, part=al):
        return ap(name, s_(a, b, st), part=part)

    def ind(win, off):
        return (win[0].indirect(off[0]), win[1] + off[1])

    def add(e, fn, outs, ins, sem=None, inc=0, emit=True):
        wr = [x for o in outs for x in o[1]]
        rd = [x for o in ins if isinstance(o, tuple) for x in o[1]]
        ops.append({"e": e, "fn": fn, "wr": wr, "rd": rd, "sem": sem, "inc": inc, "emit": emit})

    def v(x):
        return x[0] if isinstance(x, tuple) else x

    def cp(o, i):
        add("V", lambda: g.vector.tensor_copy(o[0], i[0]), [o], [i])

    def tt(o, a, b, op):
        add("V", lambda: g.vector.tensor_tensor(o[0], a[0], b[0], op), [o], [a, b])

    def ts(o, a, s1, op0, s2=None, op1=None):
        if op1 is None:
            add("V", lambda: g.vector.tensor_scalar(o[0], a[0], v(s1), None, op0), [o], [a, s1])
        else:
            add("V", lambda: g.vector.tensor_scalar(o[0], a[0], v(s1), v(s2), op0, op1), [o], [a, s1, s2])

    def ms(o, x):
        add("V", lambda: g.vector.memset(o[0], x), [o], [])

    def scan(o, d0, d1, op0, op1):
        add("V", lambda: g.vector.tensor_tensor_scan(o[0], d0[0], d1[0], 0.0, op0, op1), [o], [d0, d1])

    def act(o, i, func=ACT.Copy, scale=None, bias=None):
        kw = {}
        if scale is not None:
            kw["scale"] = v(scale)
        if bias is not None:
            kw["bias"] = v(bias)
        add("A", lambda: g.scalar.activation(o[0], i[0], func, **kw), [o], [i, scale, bias])

    def mm(o, l, r, start=True, stop=True):
        add("P", lambda: g.tensor.matmul(o[0], l[0], r[0], start, stop), [o], [l, r])

    def iota(o, pat, base, cm, flt=False):
        if flt:
            add("G", lambda: g.iota(o[0], pat, base, cm, allow_small_or_imprecise_dtypes=True), [o], [])
        else:
            add("G", lambda: g.iota(o[0], pat, base, cm), [o], [])

    def sel(o, i, pat, op, base, cm, fill=0.0):
        add("G", lambda: g.affine_select(o[0], i[0], pat, op, fill, base, cm), [o], [i])

    def dma(e, o, i):
        sem = "d%d" % ndma[0]
        ndma[0] += 1
        add(e, lambda: queue[e].dma_start(o[0], i[0]).then_inc(T.sem[sem], 16), [o], [i], sem=sem, inc=16)

    def send(sem, pairs):
        n = len(bits) // len(pairs)
        nsent[0] += len(bits)
        add("G", lambda: g.remote_dma_fused(
            [RemoteDMATransfer(dst_ids=[DstId(rid=rid, pnc=pid)], dma_engine_mask=sum(bits[n * j:n * j + n]),
                               remote_sem=T.sem[sem], src=a[0], dst=b[0]) for j, (a, b) in enumerate(pairs)],
            local_sem=T.sem.sent), [], [a for a, b in pairs], sem="sent")

    def arrive(sem, bufs):
        add("G", None, bufs, [], sem=sem, inc=8, emit=False)

    def ext(t, *idx):
        return (t[idx], [])

    def weave(main, fill):
        fill = list(fill)
        for f in main:
            f()
            if fill:
                fill.pop(0)()
        for f in fill:
            f()

    dma("A", ap("v0i"), ext(T.v0, al))
    for a, b in zip(ENCUT, ENCUT[1:]):
        dma("S", c("eni", a, b), ext(T.en, al, s_(a, b)))
    dma("S", c("LZ", 0, 256), ext(T.z0, al))
    dma("S", c("wti", 0, 1), ext(T.wt, al))
    dma("S", c("xt", 0, W), ext(T.xs, al))

    LMC, ME, MO, YI, WF, YE, YO, C16, BC = 0, 1, 2, 3, 4, 5, 6, 7, 8

    def cl(j):
        return c("col", j, j + 1)

    b8 = c("B32", 0, 128, 16)
    ms(ap("one32"), 1.0)
    iota(ap("rmi"), [[0, 16], [-1, 16]], 16, 1)
    sel(c("Bt", 0, 128), c("one32", 0, 128), [[-16, 8], [0, 16]], ALU.is_ge, 0, 1)
    sel(ap("B32"), c("Bt", 0, 128), [[16, 8], [0, 16]], ALU.is_ge, 15, -1)
    iota(c("pi", 0, 1), [[0, 1]], 0, 1)
    sel(ap("I32"), c("one32", 0, 128), [[-1, 128]], ALU.is_equal, 0, 1)
    sel(ap("tS"), ap("B32"), [[1, 128]], ALU.is_gt, 0, -1)
    iota(ap("T18"), [[0, 8], [1, 18]], -1, 0, True)
    iota(ap("repi"), [[18, 16]], 16, 0)
    iota(ap("PT0"), [[-1, 256]], 256, 0, True)

    ms(ap("onebf"), 1.0)
    ms(ap("hf"), 0.5)
    ms(ap("z144"), 0.0)
    ms(ap("ZW0"), 0.0)
    ms(ap("ZW1"), 0.0)
    ms(ap("LW"), 0.0)
    ms(c("xt", W, W + 16), 0.0)
    ms(ap("SEG"), 0.0)
    ms(ap("SG16"), 1.0)
    ms(ap("EI"), 0)
    ms(c("Acol", 0, 1), 0.0)
    ms(c("P0", 256, 512), float(W))
    ms(cl(C16), 16.0 * (W * (9 + HOPS - 1) + 2048))
    ms(c("SEG", 0, 144, 18), 1.0e9)
    ms(c("SG16", 0, 256, 16), 0.0)
    ts(ap("rmj"), ap("rmi"), 15, ALU.bitwise_and)
    ts(ap("Rm"), ap("rmj"), 0.0, ALU.is_equal)
    for r in range(16):
        if r < 12:
            act(c("Sel", 128 * r, 128 * r + 128), ap("B32"), scale=c("Rm", r, r + 1))
        else:
            ts(c("Sel", 128 * r, 128 * r + 128), ap("B32"), c("Rm", r, r + 1), ALU.mult)
    act(ap("B8k"), ap("B32"), scale=8192.0)
    act(ap("TriS"), ap("tS"), scale=8192.0)
    cp(c("LU", 0, 16), ap("v0i"))
    ts(ap("v0h"), ap("v0i"), -2048.0, ALU.add)
    cp(c("VF", 0, 16), ap("v0i"))
    ts(c("pj", 0, 1), c("pi", 0, 1), 15, ALU.bitwise_and)
    ts(c("pk", 0, 1), c("pi", 0, 1), 1, ALU.bitwise_and)
    ts(cl(LMC), c("pj", 0, 1), 4096.0, ALU.mult, 2048.0 - 17 * W, ALU.add)
    ts(cl(ME), c("pk", 0, 1), 0.0, ALU.is_equal)
    ts(cl(YI), c("pj", 0, 1), 1.0, ALU.add)
    tt(cl(MO), c("pk", 0, 1), c("Rm", 15, 16), ALU.subtract)
    for t in range(HOPS - 1):
        ts(cl(BC + t), c("Rm", 15, 16), float(W * (9 + t) + 2048), ALU.mult)
    tt(cl(YE), cl(YI), cl(ME), ALU.mult)
    tt(cl(YO), cl(YI), cl(MO), ALU.mult)

    def spread(bank, o, src):
        for r in range(16):
            mm(c(bank, o + r, o + 256, 16), c("Sel", 128 * r, 128 * r + 128), src)

    def conv(j):
        cp(c("ring", ENCUT[j], ENCUT[j + 1]), c("eni", ENCUT[j], ENCUT[j + 1]))

    def pairs(bank, eq, row, tri, start, stop, order):
        out = []
        for c1 in order:
            if c1 < 15:
                out.append(lambda c1=c1: mm(c(bank, 16 * c1 + 16, 256), ap("B8k"), ap(eq, row.start + row.step * c1, s_(16, 256 - 16 * c1)),
                                            False, start and c1 == 14))
            else:
                out.append(lambda: None)
        out.append(lambda: mm(c(bank, 0, 256), ap(tri), ap(eq, row, s_(0, 16)), start, stop and not start))
        return out[-1:] + out[:-1] if start else out

    spread("P5", 0, ap("v0h"))
    ms(ap("T18", al, 0), FAILKEY)
    ms(ap("T18", al, 17), 65536.0)
    ts(ap("Dm"), ap("Rm"), -1.0e9, ALU.mult, 1.0e9, ALU.add)
    cp(ap("repU"), ap("repi"))
    tt(ap("PT"), ap("PT0"), ap("Dm"), ALU.max)
    cp(ap("FV", 1, al), c("P5", 0, 256))
    act(ap("c1"), ap("B32"), scale=-128.0)
    sel(ap("LC"), ap("T18"), [[-16, 8], [0, 18]], ALU.is_equal, 0, 1)
    sel(ap("LC", al, s_(1, 17)), ap("LC", al, s_(1, 17)), [[-16, 8], [0, 16]], ALU.not_equal, -1, 1, 1.5 * BIG)
    sel(ap("WC"), ap("c1"), [[-1, 128]], ALU.not_equal, 0, 1, -128.0 - BIG)
    iota(ap("dW"), [[16, 32]], W, 1, True)
    for r in range(16):
        sel(c("Dg", 128 * r, 128 * r + 128), ap("I32"), [[0, 8], [1, 16]], ALU.is_equal, -r, 0)
    iota(c("VAL", 0, 256), [[-1, 256]], 320, 0, True)
    iota(c("AT", 0, W), [[0, W]], 0, 0, True)
    iota(c("VAL", 256, 256 * HOPS), [[320, HOPS - 1], [-1, 256]], 640, 0, True)
    act(ap("Ibf"), ap("I32"))
    act(ap("nIbf"), ap("I32"), scale=-1.0)

    act(ap("LW", al, s_(1, 17)), ap("I32"), ACT.Silu, scale=0.5 * BIG)
    act(ap("B32m"), b8, scale=32.0)
    act(ap("B16n"), b8, scale=-16.0)
    act(ap("B16p"), b8, scale=16.0)
    act(ap("ZW0", al, s_(1, 17)), ap("B32"), scale=-16.0)
    act(ap("ZW1", al, s_(1, 17 - NA)), c("B32", 0, 128, 16 // (16 - NA)), scale=-16.0)
    act(ap("Me"), ap("I32"), scale=cl(ME))
    act(ap("Mo"), ap("I32"), scale=cl(MO))
    act(ap("M15"), ap("I32"), scale=c("Rm", 15, 16))
    tt(c("m8", 0, 8), c("Rm", 0, 8), c("Rm", 8, 16), ALU.add)
    ts(c("m8", 8, 9), c("pj", 0, 1), 8.0, ALU.is_lt)
    ts(c("m8", 9, 10), c("pj", 0, 1), 8.0, ALU.is_ge)
    for r in range(8):
        act(c("Sel2", 128 * r, 128 * r + 128), ap("B32"), scale=c("m8", r, r + 1))

    up, down = list(range(16)), list(range(15, -1, -1))
    pm = pairs("P2", "EQ2", s_(0, 16, 1), "TriS", True, True, up)
    for c1 in up:
        ts(ap("EQ2", c1, s_(0, 256 - 16 * c1)), ap("FV", 1, s_(16 * c1, 256)), 2048.0, ALU.add, c("VF", c1, c1 + 1), ALU.is_equal)
    for f in pm:
        f()
    act(c("LZ", 256, 512), c("P2", 0, 256))
    for j in range(len(ENCUT) - 1):
        conv(j)

    ringw = c("ring", 0, W)
    xw = c("xt", 0, W + 16)

    for t in range(HOPS):
        last = t == HOPS - 1
        zc = 512 * t
        vU = 16 * t
        mU = 32 * t
        zz = c("LZ", zc, zc + 256)
        Fb, Vb = ap("FV", 2 * t, al), ap("FV", 2 * t + 1, al)
        if t > 0:
            arrive("aw%d" % t, [c("LU", vU, vU + 16), c("LH", vU, vU + 16)])
            arrive("az%d" % t, [zz, Vb])
            arrive("ad%d" % t, [c("LZ", zc + 256, zc + 512)])
            spread("P0", 256, c("LH", vU, vU + 16))

        def half(name, h, k):
            return c(name, 2048 * h + k, 2048 * h + 2048, 16)

        def blk(name, h, k, n=1):
            return c(name, 2048 * h + 128 * k, 2048 * h + 128 * (k + n))

        def hc(name, h, w=128, o=0):
            return c(name, o + w * h, o + w * h + w)

        def gat(e, dst, win, lst, a, b):
            if e == "V":
                cp(c(dst, 16 * a, 16 * b), ind(win, c(lst, a, b)))
            else:
                act(c(dst, 16 * a, 16 * b), ind(win, c(lst, a, b)))

        def ysum(a, b):
            for j in range(a, b):
                mm(c("P7", j, 256, 32), c("ring", 128 * j, 128 * j + 128), ap("Wy"))

        def z_in():
            mm(c("P1", 0, 256), ap("Ibf"), zz)
            for h in range(2):
                mm(hc("P1", h, 8, 256), hc("LZ", h, 128, zc), ap("wblk"))

        if t > 0:
            z_in()
        nop = lambda: None
        af = [nop, nop, lambda: cp(cl(WF), c("wti", 0, 1)), lambda: (ts(ap("wblk"), b8, cl(WF), ALU.mult), z_in())]
        if t > 0:
            af = [lambda: cp(c("a0", 0, 1), c("P6", 300, 301)), lambda: ts(c("a1", 0, 1), c("a0", 0, 1), 255, ALU.bitwise_and),
                  lambda: cp(c("Acol", 0, 1), c("a1", 0, 1)), lambda: cp(c("VF", 0, 16), c("LU", vU, vU + 16))]
        uf = [lambda: cp(ap("u0"), c("P1", 256, 272)), lambda: ts(ap("u1"), ap("u0"), W - 1, ALU.bitwise_and),
              lambda: tt(ap("u2"), ap("u1"), ap("u1"), ALU.mult),
              lambda: ts(ap("u3"), ap("u1"), 37.0, ALU.mult, c("Acol", 0, 1), ALU.add),
              lambda: ts(ap("u4"), ap("u2"), 5, ALU.logical_shift_right), lambda: tt(ap("u5"), ap("u3"), ap("u4"), ALU.add),
              lambda: ts(ap("u0"), ap("u5"), W - 1, ALU.bitwise_and)]
        if t == 1:
            act(ap("Wy"), b8, scale=cl(YI))
            act(ap("WyE"), ap("B32"), scale=cl(YE))
            act(ap("WyO"), ap("B32"), scale=cl(YO))
            act(ap("M16"), c("Sel", 128 * 15, 128 * 16), scale=16.0)
        act(ap("Lm"), c("P0", 256, 512), ACT.Sign, bias=cl(LMC))
        act(ap("Rv"), ind(ringw, c("LU", vU, vU + 16)))
        for j, (a, b) in enumerate(((0, 64), (64, 256))):
            cp(c("RI", a, b), ind(ringw, c("LU", vU + a // 16, vU + b // 16)))
            af[2 * j]()
            ts(c("RA", a, b), c("RI", a, b), W - 1, ALU.bitwise_and)
            af[2 * j + 1]()
            cp(c("nU", a, b), c("RA", a, b))
            gat("A", "F", ringw, "nU", a, min(b, 128 - FV0))
        nf, me, m15, mo = ("P0", "WyE", "M16", "WyO") if last else ("P7", "Me", "M15", "Mo")
        nb = "P7"

        def early_f():
            mm(c(nf, 256, 512), ap(me), ap("Rv"), True, False)
            mm(c(nf, 256, 512), ap(m15), Vb, False, False)

        def early_v():
            mm(c(nb, 0, 256), ap(mo), ap("Rv"), last, False)

        if not last:
            early_f()
            early_v()
        uf[0]()
        gat("V", "F", ringw, "nU", 128 - FV0, 128)
        uf[1]()
        gat("A", "F", ringw, "nU", 128, 256)

        def diag(h):
            mm(c("P%d" % (2 + h), 0, 144), ap("onebf"), ap("z144"), True, False)
            for k in range(16):
                mm(c("P%d" % (2 + h), 1 + k, 144, 18), half("F", h, k), c("I32", (k + t) % 16, 128, 16), False, k == 15)

        def cmps(h):
            for k in range(16):
                tt(blk("CMP", h, k), half("F", h, k), c("P0", 256 + 128 * h, 384 + 128 * h), ALU.is_ge)

        def names(h, fill):
            e3 = ap("EI", s_(8 * h, 8 * h + 8), s_(1, 17))
            weave([lambda: cp(ap("EI", s_(8 * h, 8 * h + 8), s_(0, 18)), c("P%d" % (2 + h), 0, 144)),
                   lambda: ts(hc("NA", h), e3, W - 1, ALU.bitwise_and),
                   lambda: (ts(hc("NH", h), hc("NA", h), -2048.0, ALU.add), mm(hc("P4", h), hc("NH", h), ap("Ibf")))], fill)
            ts(hc("aU", h), hc("P4", h), 2048.0, ALU.add)

        def key_z(h):
            mm(c("P%d" % (5 + h), 0, 144), hc("LZ", h, 128, zc), ap("ZW%d" % h), True, False)

        def key_open(h):
            kb = "P%d" % (5 + h)
            for k in range(16):
                mm(c(kb, 1 + k, 144, 18), blk("CMP", h, k), c("WC", (k + t) % 16, 128, 16), False, False)

        def key_x(h, n):
            for k in range(n):
                mm(c("P%d" % (5 + h), 1 + k, 144, 18), half("X", h, k), ap("B16n"), False, False)

        def key_max(h, ks, stop):
            for k in ks:
                tt(blk("MX", h, k), half("X", h, k), hc("P1", h), ALU.max)
                mm(c("P%d" % (5 + h), 1 + k, 144, 18), blk("MX", h, k), ap("B32m"), False, stop and k == ks[-1])

        def argmin(h, fill=()):
            kb = c("P%d" % (5 + h), 0, 144)
            scan(hc("run", h, 144), ap("SEG"), kb, ALU.add, ALU.min)
            fill = list(fill) + [nop] * 3
            fill[0]()
            tt(hc("ne", h, 144), kb, hc("run", h, 144), ALU.not_equal)
            fill[1]()
            scan(hc("win", h, 144), hc("ne", h, 144), hc("DE", h, 144), ALU.mult, ALU.add)
            fill[2]()
            tt(hc("MR", h), ind(c("win", 0, 144 * h + 144), c("repU", 8 * h, 8 * h + 8)), hc("Rm", h), ALU.mult)

        def wrap(h):
            mm(hc("P4", h, 8, 256), hc("MR", h), b8)

        def delta(h):
            r_ = s_(8 * h, 8 * h + 8)
            tt(hc("DE", h, 144), c("P%d" % (2 + h), 0, 144), ap("EI", r_, s_(1, 19)), ALU.subtract)

        for h in range(2):
            key_z(h)
            mm(c("P%d" % (5 + h), 0, 144), hc("Lm", h), ap("LW"), False, False)
            mm(c("P%d" % (5 + h), 0, 144), ap("onebf"), ap("LC"), False, False)
            if last and h == 0:
                ysum(0, YS0)
        diag(0)
        cmps(0)
        key_open(0)
        names(0, [uf[2], uf[3], lambda: (uf[4](), delta(0))])
        gat("A", "X", xw, "aU", 0, 128)
        if last:
            ysum(YS0, YS0 + 3)
        diag(1)
        cmps(1)
        key_open(1)
        names(1, [uf[5], uf[6], lambda: delta(1)])
        gat("A", "X", xw, "aU", 128, 256 - XV1)
        tt(c("DE", 0, 288, 18), c("DE", 0, 288, 18), ap("u0"), ALU.add)
        key_x(0, 16)
        for r in range(16):
            mm(c("P0", 0, 16), c("Dg", 128 * r, 128 * r + 128), c("LZ", zc + 256 + r, zc + 512, 16), r == 0, r == 15)
        ab = [list(range(16 - NA, 16))[:4], list(range(16 - NA, 16))[4:]]
        for j, ks in enumerate(ab):
            for i, k in enumerate(ks):
                mm(hc("P%d" % (2 + j), i), ap("nIbf"), hc("LZ", 1, 128, zc), i == 0, False)
        key_max(0, up, True)
        if last:
            ysum(YS0 + 3, 32)
        if XV1:
            gat("V", "X", xw, "aU", 256 - XV1, 256)
        argmin(0, [lambda: tt(ap("oa0"), c("P0", 0, 16), c("dW", 0, 16), ALU.min),
                   lambda: tt(ap("oa1"), ap("oa0"), c("VF", 0, 16), ALU.max), lambda: cp(ap("oaU"), ap("oa1"))])
        for j, ks in enumerate(ab):
            for i, k in enumerate(ks):
                mm(hc("P%d" % (2 + j), i), ap("Ibf"), half("X", 1, k), False, k == ks[-1])
            if ks:
                act(blk("MX", 1, ks[0], len(ks)), c("P%d" % (2 + j), 0, 128 * len(ks)), ACT.Abs)
        key_x(1, 16 - NA)
        wrap(0)
        weave([(lambda k=k: key_max(1, [k], False)) for k in range(16 - NA)],
              [nop] * (14 - NA) + [lambda: ts(c("WI", 0, 8), c("P4", 256, 264), float(W), ALU.add),
                                   lambda: ts(c("fI", 0, 8), c("WI", 0, 8), W - 1, ALU.bitwise_and),
                                   lambda: cp(c("VF", 16, 24), c("fI", 0, 8))])
        for k in range(16 - NA, 16):
            mm(c("P6", 1 + k, 144, 18), blk("MX", 1, k), ap("B16p"), False, k == 15)
        mm(c("P3", 0, 256), ap("Ibf"), c("LZ", zc + 256, zc + 512), True, False)
        mm(c("P3", 0, 256), ap("Ibf"), ap("hf"), False, False)
        pf = pairs("P3", "EQ1", s_(0, 32, 2), "TriS", False, True, up)
        pv = pairs("P3", "EQ1", s_(1, 32, 2), "TriS", False, False, up)
        if last:
            act(ap("YT"), c("P7", 0, 256))
        add("A", lambda t=t: g.scalar.activation(T.AT[:].indirect(T.oaU[:]), T.VAL[:, 256 * t:256 * t + 256], ACT.Silu),
            [ap("AT")], [ap("oaU"), c("VAL", 256 * t, 256 * t + 256)])

        def eq1(c1, a, b):
            ts(ap("EQ1", s_(2 * c1 + a, 2 * c1 + b), s_(0, 256 - 16 * c1)), ap("FV", s_(2 * t + a, 2 * t + b), s_(16 * c1, 256)),
               2048.0, ALU.add, c("VF", 16 + c1, 17 + c1), ALU.is_equal)

        def fv(c1):
            return lambda: (eq1(c1, 1, 2), pv[c1]())

        for c1 in range(FE):
            fv(c1)()
        if last:
            for h in range(2):
                mm(hc("P2", h), hc("YT", h), ap("I32"))
            act(ap("YS"), c("P2", 0, 256))
            for h in range(2):
                dma("S", (T.S[64 * h:64 * h + 64:16, 0:W], hc("S", h, W // 2)[1]), hc("YS", h))
        argmin(1, [fv(7), fv(6), fv(5)])
        wrap(1)
        for c1 in range(4, FG - 1, -1):
            fv(c1)()

        ew = c("P4", 256, 272)
        fU, zU = c("MU", mU, mU + 16), c("MU", mU + 16, mU + 32)
        ts(c("WI", 8, 16), c("P4", 264, 272), float(W), ALU.add)
        ts(zU, ew, float(W), ALU.min)
        act(ap("XF"), ind(xw, zU))
        ts(c("fI", 8, 16), c("WI", 8, 16), W - 1, ALU.bitwise_and)
        if last:
            cp(ap("EW"), ew)
        else:
            ts(ap("flag"), zU, float(W), ALU.is_lt)
        for j in range(2):
            ts(c("fH", j, 32, 2), ap("fI"), -2048.0, ALU.add, c("m8", 8 + j, 9 + j), ALU.mult)
        for r in range(8):
            mm(c("P5", r, 256, 8), c("Sel2", 128 * r, 128 * r + 128), ap("fH"))
        cp(fU, ap("fI"))
        cp(c("VF", 24, 32), c("fI", 8, 16))

        def zdiff():
            mm(c("P6", 0, 256), ap("Ibf"), zz, True, False)
            mm(c("P6", 0, 256), ap("nIbf"), ap("XF"), False, True)
            act(c("MZ", zc, zc + 256), c("P6", 0, 256), ACT.Abs)

        act(ap("YA"), ind(c("AT", 0, W), fU), ACT.Relu, bias=-float(64 + 320 * t))
        if not last:
            tt(c("MH", mU + 16, mU + 32), ap("WI"), ap("fI"), ALU.subtract)
            send("aw%d" % (t + 1), [(fU, c("LU", vU + 16, vU + 32)), (c("MH", mU + 16, mU + 32), c("LH", vU + 16, vU + 32))])
        for c1 in range(FE, FG):
            fv(c1)()
        mm(c("P3", 0, 128), ap("TriS"), ap("EQ1", s_(1, 16, 2), s_(0, 16)), False, False)
        tt(ap("DV"), ap("dW"), ap("VF"), ALU.subtract)
        zdiff()
        if last:
            act(c("RF", 0, 256), ind(ringw, fU))
        else:
            act(c("RF", 0, 256), ind(ringw, fU), scale=cl(ME))
            act(c("RF", 256, 512), ind(ringw, fU), scale=cl(MO))
        cp(Fb, c("P5", 0, 256))
        if last:
            early_v()

        if last:
            dma("S", ext(T.yz, al), c("MZ", zc, zc + 256))
        else:
            send("az%d" % (t + 1), [(c("MZ", zc, zc + 256), c("LZ", zc + 512, zc + 768)), (Fb, ap("FV", 2 * t + 3, al))])
        for c1 in range(8):
            eq1(c1, 0, 1)
            pf[c1]()
        for c1 in range(8, 16):
            eq1(c1, 0, 2)
            pf[c1]()
            pv[c1]()
        tt(ap("YZ"), ap("PT"), ap("YA"), ALU.subtract)
        mm(c("P3", 128, 256), ap("TriS"), ap("EQ1", s_(17, 32, 2), s_(0, 16)), False, False)
        pf[16]()
        mm(c(nb, 0, 256), ap(m15), Fb, False, not last)
        if last:
            mm(c("P7", 0, 256), ap("WyE"), c("RF", 0, 256), False, True)
            early_f()
            mm(c("P0", 256, 512), ap("WyO"), c("RF", 0, 256), False, True)
            act(c("AB", 0, 256), c("P7", 0, 256), ACT.Identity, bias=cl(C16))
            act(c("AB", 256, 512), c("P0", 256, 512), ACT.Identity, bias=cl(C16))
            for r in range(16):
                mm(c("P1", r, 256, 16, part=s_(0, 8)), c("I32", r, 128, 16), ap("EW"))
            act(ap("YP", part=s_(0, 8)), c("P1", 0, 256, part=s_(0, 8)))
            dma("A", ext(T.yp, al), ap("YP", part=s_(0, 8)))
        else:
            act(ap("AB"), c("P7", 0, 512), ACT.Identity, bias=cl(BC + t))
            for f in pairs("P2", "EQ1", s_(0, 32, 2), "TriS", True, True, up):
                f()
            act(c("MZ", zc + 256, zc + 512), c("P2", 0, 256))
            send("ad%d" % (t + 1), [(c("MZ", zc + 256, zc + 512), c("LZ", zc + 768, zc + 1024))])
            for j in range(16):
                mm(c("P6", 300, 301), ap("onebf"), c("flag", j, j + 1), j == 0, j == 15)
        tt(ap("O1"), c("P3", 0, 256), ap("YZ"), ALU.is_gt)
        scan(ap("bd"), ap("SG16"), ap("O1"), ALU.mult, ALU.add)
        for h in range(2):
            tt(hc("bd2", h, 16), c("bd", 15, 256, 16), hc("DV", h, 16), ALU.mult)
        tt(ap("off"), ap("bd2"), ap("VF"), ALU.add)
        cp(ap("offU"), ap("off"))
        if last:
            for h in range(2):
                add("V", lambda h=h: g.vector.tensor_copy(T.S[:].indirect(T.offU[:, 16 * h:16 * h + 16]), T.AB[:, 256 * h:256 * h + 256]),
                    [ap("S")], [ap("offU"), hc("AB", h, 256)])
            dma("S", ext(T.ys, al), c("S", 0, W, part=s_(0, 128, 16)))
        else:
            add("V", lambda: g.vector.tensor_tensor(T.ring[:].indirect(T.offU[:]), T.RF[:], T.AB[:], ALU.add),
                [ap("ring")], [ap("offU"), ap("RF"), ap("AB")])

    hist = {}
    deps = []
    for i, o in enumerate(ops):
        d = set()
        for kind in ("rd", "wr"):
            for name, m in o[kind]:
                ps = SCRATCH[name][0] == "psum"
                for j, e2, w2, m2 in hist.get(name, []):
                    if j == i or not (m & m2):
                        continue
                    if ps:
                        if e2 != o["e"] or (w2 and e2 != "P"):
                            d.add(j)
                    elif w2 or kind == "wr":
                        d.add(j)
        for kind in ("rd", "wr"):
            for name, m in o[kind]:
                h_ = hist.setdefault(name, [])
                if kind == "wr":
                    h_[:] = [x for x in h_ if (x[3] & ~m) or x[0] == i]
                elif m == -1:
                    h_[:] = [x for x in h_ if x[1] == o["e"]][-1:]
                h_.append((i, o["e"], kind == "wr", m))
        top = {}
        for j in d:
            key = ops[j]["sem"] or ops[j]["e"]
            top[key] = max(top.get(key, -1), j)
        deps.append(top)
    seen = {}
    need = set()
    for i, o in enumerate(ops):
        s = seen.setdefault(o["e"], {})
        keep = {}
        for key, j in deps[i].items():
            if s.get(key, -1) < j:
                s[key] = j
                keep[key] = j
                need.add(j)
        deps[i] = keep
    count = {}
    at = {}
    for i, o in enumerate(ops):
        if o["sem"] is None and i in need:
            count[o["e"]] = count.get(o["e"], 0) + 1
            at[i] = count[o["e"]]
    for i, o in enumerate(ops):
        if not o["emit"]:
            continue
        qu = queue[o["e"]]
        for key, j in deps[i].items():
            if ops[j]["sem"] is None:
                qu.wait_ge(T.sem["e" + key], at[j])
            else:
                qu.wait_ge(T.sem[key], ops[j]["inc"])
        ins = o["fn"]()
        if i in at:
            ins.then_inc(T.sem["e" + o["e"]], 1)
    for i, o in enumerate(ops):
        if o["inc"] == 16 and i not in need:
            queue[o["e"]].wait_ge(T.sem[o["sem"]], 16)
    g.wait_ge(T.sem.sent, nsent[0])
